import numpy as np
import ml_dtypes


def mxq(x, axis, fmt="e4m3"):
    dtype, down = {"e4m3": (ml_dtypes.float8_e4m3fn, 7), "e5m2": (ml_dtypes.float8_e5m2, 14)}[fmt]
    v = np.moveaxis(np.asarray(x, np.float32).astype(ml_dtypes.bfloat16).astype(np.float64), axis, -1)
    blocks = v.reshape(v.shape[:-1] + (-1, 32))
    amax = np.abs(blocks).max(-1, keepdims=True)
    byte = np.maximum(np.where(amax > 0, np.frexp(amax)[1] - 1 + 127, 0) - down, 1)
    scale = np.exp2(byte - 127.0)
    codes = (blocks / scale).astype(np.float32).astype(dtype).astype(np.float64)
    return np.moveaxis((codes * scale).reshape(v.shape), -1, axis)


WIDE = False


def mx_kscale(k):
    if not WIDE:
        return np.ones(k)
    levels = np.array([10, -10, 5, -5, 0])
    if k % 512:
        return np.exp2(np.random.permutation(np.resize(levels, k // 32))).repeat(32)
    a = np.empty((k // 512, 16))
    for p in range(k // 512):
        a[p, :8] = np.random.permutation(np.resize(levels, 8))
        for g in range(8):
            far = levels[np.abs(levels - a[p, g]) >= 10]
            a[p, g + 8] = far[np.random.randint(len(far))]
    return np.exp2(a.ravel()).repeat(32)


def f64(x):
    return np.asarray(x).astype(np.float64)


def striped(idx):
    return np.tile(idx.reshape(-1, 16).T, (8, 1)).astype(np.uint16)


def unstriped(offs):
    return offs[:16].T.reshape(-1).astype(np.int64)


K, T, S, N, U = 1024, 2048, 512, 256, 1024


def setup_inputs():
    n = np.random.standard_normal
    s = mx_kscale(K)[:, None]
    return {
        "xT": (n((K, T)) * s).astype(np.float32),
        "w1": (n((K, N)) / np.sqrt(K) / s).astype(np.float32),
        "gamma": np.random.uniform(0.5, 1.5, (N, U)).astype(np.float32),
        "beta": (0.5 * n((N, U))).astype(np.float32),
        "offs": striped(np.random.permutation(T)[:S]),
        "cls": striped(np.random.randint(0, U, S)),
    }


def reference(xT, w1, gamma, beta, offs, cls):
    xq = mxq(f64(xT)[:, unstriped(offs)], 0, "e4m3")
    y = mxq(f64(w1), 0, "e4m3").T @ xq
    g = f64(gamma)[:, unstriped(cls)]
    s = f64(beta)[:, unstriped(cls)]
    return y * g + s

@@ -1,0 +1,94 @@
+from contextlib import ExitStack
+
+import concourse.mybir as mybir
+
+K, T, S, N, U = 1024, 2048, 512, 256, 1024
+FLOPS = 2 * K * N * S
+
+F32 = mybir.dt.float32
+BF16 = mybir.dt.bfloat16
+U32 = mybir.dt.uint32
+U16 = mybir.dt.uint16
+U8 = mybir.dt.uint8
+FP8X4 = mybir.dt.float8_e4m3fn_x4
+MULT = mybir.AluOpType.mult
+ADD = mybir.AluOpType.add
+
+P = 128
+PACK = 4
+K_PASS = P * PACK
+PASSES = K // K_PASS
+BLOCKS = N // P
+LIST_COLS = S // 16
+
+
+def tile_picked_cbn_none_e_kernel(tc, xT, w1, gamma, beta, offs, cls, out):
+    nc = tc.nc
+    with ExitStack() as ctx:
+        keep = ctx.enter_context(tc.tile_pool(name="keep", bufs=1))
+        psum = ctx.enter_context(tc.psum_pool(name="psum", bufs=1))
+
+        offs_t = keep.tile([P, LIST_COLS], U16, name="offs_t")
+        cls_t = keep.tile([P, LIST_COLS], U16, name="cls_t")
+        x_rows = xT.rearrange("(g p t) c -> g t p c", p=P, t=PACK)
+        w_rows = w1.rearrange("(g p t) n -> g p t n", p=P, t=PACK)
+        x_raw = [[keep.tile([P, T], F32, name="x_raw%d_%d" % (g, t)) for t in range(PACK)] for g in range(PASSES)]
+        w_raw = [keep.tile([P, PACK, N], F32, name="w_raw%d" % g) for g in range(PASSES)]
+        g_raw = [keep.tile([P, U], F32, name="g_raw%d" % b) for b in range(BLOCKS)]
+        b_raw = [keep.tile([P, U], F32, name="b_raw%d" % b) for b in range(BLOCKS)]
+
+        nc.sync.dma_start(x_raw[0][0][:], x_rows[0, 0])
+        nc.sync.dma_start(offs_t[:], offs)
+        nc.sync.dma_start(cls_t[:], cls)
+        nc.sync.dma_start(w_raw[0][:], w_rows[0])
+        for g in range(PASSES):
+            for t in range(PACK):
+                if g + t > 0:
+                    nc.sync.dma_start(x_raw[g][t][:], x_rows[g, t])
+        nc.sync.dma_start(w_raw[1][:], w_rows[1])
+        for b in range(BLOCKS):
+            nc.sync.dma_start(g_raw[b][:], gamma[b * P : (b + 1) * P, :])
+            nc.sync.dma_start(b_raw[b][:], beta[b * P : (b + 1) * P, :])
+
+        acc = [psum.tile([P, S], F32, name="acc%d" % b) for b in range(BLOCKS)]
+        for g in range(PASSES):
+            x_bf = keep.tile([P, S, PACK], BF16, name="x_bf%d" % g, align_bytes=64)
+            for t in range(PACK):
+                nc.vector.tensor_copy(x_bf[:, :, t], x_raw[g][t][:].indirect(offs_t[:]))
+            x_codes = keep.tile([P, S], U32, name="x_codes%d" % g, align_bytes=64)
+            x_scales = keep.tile([P, S], U8, name="x_scales%d" % g, align_bytes=64)
+            nc.vector.quantize_mx(x_codes[:].bitcast(FP8X4), x_scales[:], x_bf[:].rearrange("p s t -> p (s t)"))
+
+            w_bf = keep.tile([P, N, PACK], BF16, name="w_bf%d" % g, tag="w_bf%d" % g, align_bytes=64)
+            nc.scalar.copy(
+                w_bf[:].rearrange("p (c i) t -> p c t i", i=4),
+                w_raw[g][:].rearrange("p t (c i) -> p c t i", i=4),
+            )
+            w_codes = keep.tile([P, N], U32, name="w_codes%d" % g, align_bytes=64)
+            w_scales = keep.tile([P, N], U8, name="w_scales%d" % g, align_bytes=64)
+            nc.vector.quantize_mx(w_codes[:].bitcast(FP8X4), w_scales[:], w_bf[:].rearrange("p n t -> p (n t)"))
+            for b in range(BLOCKS):
+                cols = slice(b * P, (b + 1) * P)
+                nc.tensor.matmul_mx(
+                    out=acc[b][:],
+                    lhsT=w_codes[:, cols].bitcast(FP8X4),
+                    lhsT_scale=w_scales[:, cols],
+                    rhs=x_codes[:].bitcast(FP8X4),
+                    rhs_scale=x_scales[:],
+                    start=(g == 0),
+                    stop=(g == PASSES - 1),
+                )
+
+        g_picked = keep.tile([P, S], F32, name="g_picked", tag="w_bf%d" % (PASSES - 1), align_bytes=64)
+        nc.vector.tensor_copy(g_picked[:], g_raw[0][:].indirect(cls_t[:]))
+        y_last = keep.tile([P, S], F32, name="y_last")
+        nc.scalar.copy(y_last[:], acc[1][:])
+        for b in range(BLOCKS):
+            scaled = keep.tile([P, S], F32, name="scaled%d" % b)
+            if b == 0:
+                nc.vector.tensor_tensor(scaled[:], acc[0][:], g_picked[:], MULT)
+            else:
+                nc.vector.tensor_tensor(scaled[:], g_raw[b][:].indirect(cls_t[:]), y_last[:], MULT)
+            result = keep.tile([P, S], F32, name="result%d" % b)
+            nc.vector.tensor_tensor(result[:], b_raw[b][:].indirect(cls_t[:]), scaled[:], ADD)
+            nc.sync.dma_start(out[b * P : (b + 1) * P, :], result[:])

@@ -20,6 +20,8 @@ K_PASS = P * PACK
 PASSES = K // K_PASS
 BLOCKS = N // P
 LIST_COLS = S // 16
+HALVES = 2
+H = S // HALVES
 
 
 def tile_picked_cbn_none_e_kernel(tc, xT, w1, gamma, beta, offs, cls, out):
@@ -30,35 +32,35 @@ def tile_picked_cbn_none_e_kernel(tc, xT, w1, gamma, beta, offs, cls, out):
 
         offs_t = keep.tile([P, LIST_COLS], U16, name="offs_t")
         cls_t = keep.tile([P, LIST_COLS], U16, name="cls_t")
-        x_rows = xT.rearrange("(g p t) c -> g t p c", p=P, t=PACK)
+        x_rows = xT.rearrange("(g p t) c -> g p t c", p=P, t=PACK)
         w_rows = w1.rearrange("(g p t) n -> g p t n", p=P, t=PACK)
-        x_raw = [[keep.tile([P, T], F32, name="x_raw%d_%d" % (g, t)) for t in range(PACK)] for g in range(PASSES)]
         w_raw = [keep.tile([P, PACK, N], F32, name="w_raw%d" % g) for g in range(PASSES)]
         g_raw = [keep.tile([P, U], F32, name="g_raw%d" % b) for b in range(BLOCKS)]
         b_raw = [keep.tile([P, U], F32, name="b_raw%d" % b) for b in range(BLOCKS)]
 
-        nc.sync.dma_start(x_raw[0][0][:], x_rows[0, 0])
-        nc.sync.dma_start(offs_t[:], offs)
-        nc.sync.dma_start(cls_t[:], cls)
-        nc.sync.dma_start(w_raw[0][:], w_rows[0])
-        for g in range(PASSES):
-            for t in range(PACK):
-                if g + t > 0:
-                    nc.sync.dma_start(x_raw[g][t][:], x_rows[g, t])
+        loads = [(0, 0, 2), (0, 2, 2), (1, 0, 1), (1, 1, 1), (1, 2, 1), (1, 3, 1)]
+        plane = {}
+        for g, t0, rows in loads:
+            x_raw = keep.tile([P, rows * T], F32, name="x_raw%d_%d" % (g, t0), tag="x_raw%d_%d" % (g, t0), align_bytes=64)
+            nc.sync.dma_start(x_raw[:], x_rows[g, :, t0 : t0 + rows, :].rearrange("p t c -> p (t c)"))
+            for i in range(rows):
+                plane[g, t0 + i] = x_raw[:, i * T : (i + 1) * T]
+            if (g, t0) == (0, 0):
+                nc.sync.dma_start(offs_t[:], offs)
+                nc.sync.dma_start(cls_t[:], cls)
+                nc.sync.dma_start(w_raw[0][:], w_rows[0])
         nc.sync.dma_start(w_raw[1][:], w_rows[1])
         for b in range(BLOCKS):
             nc.sync.dma_start(g_raw[b][:], gamma[b * P : (b + 1) * P, :])
             nc.sync.dma_start(b_raw[b][:], beta[b * P : (b + 1) * P, :])
 
-        acc = [psum.tile([P, S], F32, name="acc%d" % b) for b in range(BLOCKS)]
-        for g in range(PASSES):
-            x_bf = keep.tile([P, S, PACK], BF16, name="x_bf%d" % g, align_bytes=64)
-            for t in range(PACK):
-                nc.vector.tensor_copy(x_bf[:, :, t], x_raw[g][t][:].indirect(offs_t[:]))
-            x_codes = keep.tile([P, S], U32, name="x_codes%d" % g, align_bytes=64)
-            x_scales = keep.tile([P, S], U8, name="x_scales%d" % g, align_bytes=64)
-            nc.vector.quantize_mx(x_codes[:].bitcast(FP8X4), x_scales[:], x_bf[:].rearrange("p s t -> p (s t)"))
+        half = [slice(h * H, (h + 1) * H) for h in range(HALVES)]
+        offs_h = [offs_t[:, h * H // 16 : (h + 1) * H // 16] for h in range(HALVES)]
+        cls_h = [cls_t[:, h * H // 16 : (h + 1) * H // 16] for h in range(HALVES)]
 
+        acc = [psum.tile([P, S], F32, name="acc%d" % b) for b in range(BLOCKS)]
+
+        def quantise_w(g):
             w_bf = keep.tile([P, N, PACK], BF16, name="w_bf%d" % g, tag="w_bf%d" % g, align_bytes=64)
             nc.scalar.copy(
                 w_bf[:].rearrange("p (c i) t -> p c t i", i=4),
@@ -67,6 +69,9 @@ def tile_picked_cbn_none_e_kernel(tc, xT, w1, gamma, beta, offs, cls, out):
             w_codes = keep.tile([P, N], U32, name="w_codes%d" % g, align_bytes=64)
             w_scales = keep.tile([P, N], U8, name="w_scales%d" % g, align_bytes=64)
             nc.vector.quantize_mx(w_codes[:].bitcast(FP8X4), w_scales[:], w_bf[:].rearrange("p n t -> p (n t)"))
+            return w_codes, w_scales
+
+        def multiply(g, w_codes, w_scales, x_codes, x_scales):
             for b in range(BLOCKS):
                 cols = slice(b * P, (b + 1) * P)
                 nc.tensor.matmul_mx(
@@ -79,16 +84,49 @@ def tile_picked_cbn_none_e_kernel(tc, xT, w1, gamma, beta, offs, cls, out):
                     stop=(g == PASSES - 1),
                 )
 
+        w_first = quantise_w(0)
+        x_picked = keep.tile([P, PACK, S], F32, name="x_picked")
+        for t in range(PACK):
+            nc.vector.tensor_copy(x_picked[:, t, :], plane[0, t].indirect(offs_t[:]))
+        x_bf_first = keep.tile([P, S, PACK], BF16, name="x_bf_first", align_bytes=64)
+        nc.scalar.copy(
+            x_bf_first[:].rearrange("p (c i) t -> p c t i", i=4),
+            x_picked[:].rearrange("p t (c i) -> p c t i", i=4),
+        )
+
+        x_bf = [keep.tile([P, H, PACK], BF16, name="x_bf_last%d" % h, align_bytes=64) for h in range(HALVES)]
+        for t in range(PACK):
+            for h in range(HALVES):
+                nc.vector.tensor_copy(x_bf[h][:, :, t], plane[1, t].indirect(offs_h[h]))
+            if t == 1:
+                x_codes = keep.tile([P, S], U32, name="x_codes0", tag="x_raw1_1", align_bytes=64)
+                x_scales = keep.tile([P, S], U8, name="x_scales0", align_bytes=64)
+                nc.vector.quantize_mx(
+                    x_codes[:].bitcast(FP8X4), x_scales[:], x_bf_first[:].rearrange("p s t -> p (s t)")
+                )
+                multiply(0, w_first[0], w_first[1], x_codes, x_scales)
+        x_codes = keep.tile([P, S], U32, name="x_codes1", align_bytes=64)
+        x_scales = keep.tile([P, S], U8, name="x_scales1", align_bytes=64)
+        for h in range(HALVES):
+            nc.vector.quantize_mx(
+                x_codes[:, half[h]].bitcast(FP8X4), x_scales[:, half[h]], x_bf[h][:].rearrange("p s t -> p (s t)")
+            )
+        w_last = quantise_w(1)
+        multiply(1, w_last[0], w_last[1], x_codes, x_scales)
+
         g_picked = keep.tile([P, S], F32, name="g_picked", tag="w_bf%d" % (PASSES - 1), align_bytes=64)
-        nc.vector.tensor_copy(g_picked[:], g_raw[0][:].indirect(cls_t[:]))
+        for h in range(HALVES):
+            nc.vector.tensor_copy(g_picked[:, half[h]], g_raw[0][:].indirect(cls_h[h]))
         y_last = keep.tile([P, S], F32, name="y_last")
         nc.scalar.copy(y_last[:], acc[1][:])
         for b in range(BLOCKS):
             scaled = keep.tile([P, S], F32, name="scaled%d" % b)
-            if b == 0:
-                nc.vector.tensor_tensor(scaled[:], acc[0][:], g_picked[:], MULT)
-            else:
-                nc.vector.tensor_tensor(scaled[:], g_raw[b][:].indirect(cls_t[:]), y_last[:], MULT)
+            for h in range(HALVES):
+                if b == 0:
+                    nc.vector.tensor_tensor(scaled[:, half[h]], acc[0][:, half[h]], g_picked[:, half[h]], MULT)
+                else:
+                    nc.vector.tensor_tensor(scaled[:, half[h]], g_raw[b][:].indirect(cls_h[h]), y_last[:, half[h]], MULT)
             result = keep.tile([P, S], F32, name="result%d" % b)
-            nc.vector.tensor_tensor(result[:], b_raw[b][:].indirect(cls_t[:]), scaled[:], ADD)
-            nc.sync.dma_start(out[b * P : (b + 1) * P, :], result[:])
+            for h in range(HALVES):
+                nc.vector.tensor_tensor(result[:, half[h]], b_raw[b][:].indirect(cls_h[h]), scaled[:, half[h]], ADD)
+                nc.sync.dma_start(out[b * P : (b + 1) * P, half[h]], result[:, half[h]])

@@ -48,8 +48,8 @@ def tile_picked_cbn_none_e_kernel(tc, xT, w1, gamma, beta, offs, cls, out):
             if (g, t0) == (0, 0):
                 nc.sync.dma_start(offs_t[:], offs)
                 nc.sync.dma_start(cls_t[:], cls)
-                nc.sync.dma_start(w_raw[0][:], w_rows[0])
-        nc.sync.dma_start(w_raw[1][:], w_rows[1])
+        for g in range(PASSES):
+            nc.sync.dma_start(w_raw[g][:], w_rows[g])
         for b in range(BLOCKS):
             nc.sync.dma_start(g_raw[b][:], gamma[b * P : (b + 1) * P, :])
             nc.sync.dma_start(b_raw[b][:], beta[b * P : (b + 1) * P, :])
@@ -58,33 +58,6 @@ def tile_picked_cbn_none_e_kernel(tc, xT, w1, gamma, beta, offs, cls, out):
         offs_h = [offs_t[:, h * H // 16 : (h + 1) * H // 16] for h in range(HALVES)]
         cls_h = [cls_t[:, h * H // 16 : (h + 1) * H // 16] for h in range(HALVES)]
 
-        acc = [psum.tile([P, S], F32, name="acc%d" % b) for b in range(BLOCKS)]
-
-        def quantise_w(g):
-            w_bf = keep.tile([P, N, PACK], BF16, name="w_bf%d" % g, tag="w_bf%d" % g, align_bytes=64)
-            nc.scalar.copy(
-                w_bf[:].rearrange("p (c i) t -> p c t i", i=4),
-                w_raw[g][:].rearrange("p t (c i) -> p c t i", i=4),
-            )
-            w_codes = keep.tile([P, N], U32, name="w_codes%d" % g, align_bytes=64)
-            w_scales = keep.tile([P, N], U8, name="w_scales%d" % g, align_bytes=64)
-            nc.vector.quantize_mx(w_codes[:].bitcast(FP8X4), w_scales[:], w_bf[:].rearrange("p n t -> p (n t)"))
-            return w_codes, w_scales
-
-        def multiply(g, w_codes, w_scales, x_codes, x_scales):
-            for b in range(BLOCKS):
-                cols = slice(b * P, (b + 1) * P)
-                nc.tensor.matmul_mx(
-                    out=acc[b][:],
-                    lhsT=w_codes[:, cols].bitcast(FP8X4),
-                    lhsT_scale=w_scales[:, cols],
-                    rhs=x_codes[:].bitcast(FP8X4),
-                    rhs_scale=x_scales[:],
-                    start=(g == 0),
-                    stop=(g == PASSES - 1),
-                )
-
-        w_first = quantise_w(0)
         x_picked = keep.tile([P, PACK, S], F32, name="x_picked")
         for t in range(PACK):
             nc.vector.tensor_copy(x_picked[:, t, :], plane[0, t].indirect(offs_t[:]))
@@ -94,39 +67,76 @@ def tile_picked_cbn_none_e_kernel(tc, xT, w1, gamma, beta, offs, cls, out):
             x_picked[:].rearrange("p t (c i) -> p c t i", i=4),
         )
 
+        x_codes = []
+        x_scales = []
         x_bf = [keep.tile([P, H, PACK], BF16, name="x_bf_last%d" % h, align_bytes=64) for h in range(HALVES)]
         for t in range(PACK):
             for h in range(HALVES):
                 nc.vector.tensor_copy(x_bf[h][:, :, t], plane[1, t].indirect(offs_h[h]))
             if t == 1:
-                x_codes = keep.tile([P, S], U32, name="x_codes0", tag="x_raw1_1", align_bytes=64)
-                x_scales = keep.tile([P, S], U8, name="x_scales0", align_bytes=64)
+                x_codes.append(keep.tile([P, S], U32, name="x_codes0", tag="x_raw1_1", align_bytes=64))
+                x_scales.append(keep.tile([P, S], U8, name="x_scales0", align_bytes=64))
                 nc.vector.quantize_mx(
-                    x_codes[:].bitcast(FP8X4), x_scales[:], x_bf_first[:].rearrange("p s t -> p (s t)")
+                    x_codes[0][:].bitcast(FP8X4), x_scales[0][:], x_bf_first[:].rearrange("p s t -> p (s t)")
                 )
-                multiply(0, w_first[0], w_first[1], x_codes, x_scales)
-        x_codes = keep.tile([P, S], U32, name="x_codes1", align_bytes=64)
-        x_scales = keep.tile([P, S], U8, name="x_scales1", align_bytes=64)
+        x_codes.append(keep.tile([P, S], U32, name="x_codes1", align_bytes=64))
+        x_scales.append(keep.tile([P, S], U8, name="x_scales1", align_bytes=64))
         for h in range(HALVES):
             nc.vector.quantize_mx(
-                x_codes[:, half[h]].bitcast(FP8X4), x_scales[:, half[h]], x_bf[h][:].rearrange("p s t -> p (s t)")
+                x_codes[1][:, half[h]].bitcast(FP8X4),
+                x_scales[1][:, half[h]],
+                x_bf[h][:].rearrange("p s t -> p (s t)"),
             )
-        w_last = quantise_w(1)
-        multiply(1, w_last[0], w_last[1], x_codes, x_scales)
 
-        g_picked = keep.tile([P, S], F32, name="g_picked", tag="w_bf%d" % (PASSES - 1), align_bytes=64)
-        for h in range(HALVES):
-            nc.vector.tensor_copy(g_picked[:, half[h]], g_raw[0][:].indirect(cls_h[h]))
-        y_last = keep.tile([P, S], F32, name="y_last")
-        nc.scalar.copy(y_last[:], acc[1][:])
+        w_codes = []
+        w_scales = []
+        for g in range(PASSES):
+            w_bf = keep.tile([P, N, PACK], BF16, name="w_bf%d" % g, align_bytes=64)
+            woven = w_bf[:].rearrange("p (c i) t -> p c t i", i=4)
+            rows = w_raw[g][:].rearrange("p t (c i) -> p c t i", i=4)
+            if g < PASSES - 1:
+                nc.scalar.copy(woven, rows)
+            else:
+                nc.scalar.copy(woven[:, : N // 8], rows[:, : N // 8])
+                nc.vector.tensor_copy(woven[:, N // 8 :], rows[:, N // 8 :])
+            w_codes.append(keep.tile([P, N], U32, name="w_codes%d" % g, align_bytes=64))
+            w_scales.append(keep.tile([P, N], U8, name="w_scales%d" % g, align_bytes=64))
+            nc.vector.quantize_mx(w_codes[g][:].bitcast(FP8X4), w_scales[g][:], w_bf[:].rearrange("p n t -> p (n t)"))
+
+        y = {}
         for b in range(BLOCKS):
-            scaled = keep.tile([P, S], F32, name="scaled%d" % b)
+            cols = slice(b * P, (b + 1) * P)
             for h in range(HALVES):
-                if b == 0:
-                    nc.vector.tensor_tensor(scaled[:, half[h]], acc[0][:, half[h]], g_picked[:, half[h]], MULT)
+                acc = psum.tile([P, H], F32, name="acc%d_%d" % (b, h), tag="acc%d" % h)
+                for g in range(PASSES):
+                    nc.tensor.matmul_mx(
+                        out=acc[:],
+                        lhsT=w_codes[g][:, cols].bitcast(FP8X4),
+                        lhsT_scale=w_scales[g][:, cols],
+                        rhs=x_codes[g][:, half[h]].bitcast(FP8X4),
+                        rhs_scale=x_scales[g][:, half[h]],
+                        start=(g == 0),
+                        stop=(g == PASSES - 1),
+                    )
+                if (b, h) == (BLOCKS - 1, 0):
+                    y[b, h] = acc
                 else:
-                    nc.vector.tensor_tensor(scaled[:, half[h]], g_raw[b][:].indirect(cls_h[h]), y_last[:, half[h]], MULT)
+                    y[b, h] = keep.tile([P, H], F32, name="y%d_%d" % (b, h))
+                    nc.scalar.copy(y[b, h][:], acc[:])
+
+        for b in range(BLOCKS):
+            g_picked = keep.tile([P, S], F32, name="g_picked%d" % b)
+            b_picked = keep.tile([P, S], F32, name="b_picked%d" % b)
+            scaled = keep.tile([P, S], F32, name="scaled%d" % b)
             result = keep.tile([P, S], F32, name="result%d" % b)
             for h in range(HALVES):
-                nc.vector.tensor_tensor(result[:, half[h]], b_raw[b][:].indirect(cls_h[h]), scaled[:, half[h]], ADD)
+                nc.vector.tensor_copy(g_picked[:, half[h]], g_raw[b][:].indirect(cls_h[h]))
+            for h in range(HALVES):
+                nc.vector.tensor_copy(b_picked[:, half[h]], b_raw[b][:].indirect(cls_h[h]))
+            for h in range(HALVES):
+                scaler = nc.vector if (b, h) == (BLOCKS - 1, 0) else nc.gpsimd
+                scaler.tensor_tensor(scaled[:, half[h]], y[b, h][:], g_picked[:, half[h]], MULT)
+            adder = nc.vector if b == BLOCKS - 1 else nc.gpsimd
+            for h in range(HALVES):
+                adder.tensor_tensor(result[:, half[h]], b_picked[:, half[h]], scaled[:, half[h]], ADD)
                 nc.sync.dma_start(out[b * P : (b + 1) * P, half[h]], result[:, half[h]])

@@ -22,6 +22,7 @@ BLOCKS = N // P
 LIST_COLS = S // 16
 HALVES = 2
 H = S // HALVES
+Q = H // 2
 
 
 def tile_picked_cbn_none_e_kernel(tc, xT, w1, gamma, beta, offs, cls, out):
@@ -88,55 +89,52 @@ def tile_picked_cbn_none_e_kernel(tc, xT, w1, gamma, beta, offs, cls, out):
                 x_bf[h][:].rearrange("p s t -> p (s t)"),
             )
 
-        w_codes = []
-        w_scales = []
+        w_codes = {}
+        w_scales = {}
         for g in range(PASSES):
-            w_bf = keep.tile([P, N, PACK], BF16, name="w_bf%d" % g, align_bytes=64)
-            woven = w_bf[:].rearrange("p (c i) t -> p c t i", i=4)
-            rows = w_raw[g][:].rearrange("p t (c i) -> p c t i", i=4)
-            if g < PASSES - 1:
-                nc.scalar.copy(woven, rows)
-            else:
-                nc.scalar.copy(woven[:, : N // 8], rows[:, : N // 8])
-                nc.vector.tensor_copy(woven[:, N // 8 :], rows[:, N // 8 :])
-            w_codes.append(keep.tile([P, N], U32, name="w_codes%d" % g, align_bytes=64))
-            w_scales.append(keep.tile([P, N], U8, name="w_scales%d" % g, align_bytes=64))
-            nc.vector.quantize_mx(w_codes[g][:].bitcast(FP8X4), w_scales[g][:], w_bf[:].rearrange("p n t -> p (n t)"))
+            for b in range(BLOCKS):
+                w_bf = keep.tile([P, P, PACK], BF16, name="w_bf%d_%d" % (g, b), align_bytes=64)
+                woven = w_bf[:].rearrange("p (c i) t -> p c t i", i=4)
+                rows = w_raw[g][:, :, b * P : (b + 1) * P].rearrange("p t (c i) -> p c t i", i=4)
+                if (g, b) == (PASSES - 1, 0):
+                    nc.vector.tensor_copy(woven, rows)
+                else:
+                    nc.scalar.copy(woven, rows)
+                w_codes[g, b] = keep.tile([P, P], U32, name="w_codes%d_%d" % (g, b), align_bytes=64)
+                w_scales[g, b] = keep.tile([P, P], U8, name="w_scales%d_%d" % (g, b), align_bytes=64)
+                nc.vector.quantize_mx(
+                    w_codes[g, b][:].bitcast(FP8X4), w_scales[g, b][:], w_bf[:].rearrange("p n t -> p (n t)")
+                )
 
-        y = {}
+        g_picked = [keep.tile([P, Q], F32, name="g_picked%d" % q, tag="g_picked%d" % q) for q in range(2)]
+        for q in range(2):
+            nc.vector.tensor_copy(g_picked[q][:], g_raw[0][:].indirect(cls_t[:, q * Q // 16 : (q + 1) * Q // 16]))
+
         for b in range(BLOCKS):
-            cols = slice(b * P, (b + 1) * P)
+            scaled = []
             for h in range(HALVES):
                 acc = psum.tile([P, H], F32, name="acc%d_%d" % (b, h), tag="acc%d" % h)
                 for g in range(PASSES):
                     nc.tensor.matmul_mx(
                         out=acc[:],
-                        lhsT=w_codes[g][:, cols].bitcast(FP8X4),
-                        lhsT_scale=w_scales[g][:, cols],
+                        lhsT=w_codes[g, b][:].bitcast(FP8X4),
+                        lhsT_scale=w_scales[g, b][:],
                         rhs=x_codes[g][:, half[h]].bitcast(FP8X4),
                         rhs_scale=x_scales[g][:, half[h]],
                         start=(g == 0),
                         stop=(g == PASSES - 1),
                     )
-                if (b, h) == (BLOCKS - 1, 0):
-                    y[b, h] = acc
+                if (b, h) == (0, 0):
+                    scaled.append(keep.tile([P, H], F32, name="scaled0_0"))
+                    for q in range(2):
+                        part = slice(q * Q, (q + 1) * Q)
+                        nc.vector.tensor_tensor(scaled[h][:, part], acc[:, part], g_picked[q][:], MULT)
                 else:
-                    y[b, h] = keep.tile([P, H], F32, name="y%d_%d" % (b, h))
-                    nc.scalar.copy(y[b, h][:], acc[:])
-
-        for b in range(BLOCKS):
-            g_picked = keep.tile([P, S], F32, name="g_picked%d" % b)
-            b_picked = keep.tile([P, S], F32, name="b_picked%d" % b)
-            scaled = keep.tile([P, S], F32, name="scaled%d" % b)
-            result = keep.tile([P, S], F32, name="result%d" % b)
+                    scaled.append(keep.tile([P, H], F32, name="scaled%d_%d" % (b, h)))
+                    y = keep.tile([P, H], F32, name="y%d_%d" % (b, h))
+                    nc.scalar.copy(y[:], acc[:])
+                    nc.vector.tensor_tensor(scaled[h][:], g_raw[b][:].indirect(cls_h[h]), y[:], MULT)
             for h in range(HALVES):
-                nc.vector.tensor_copy(g_picked[:, half[h]], g_raw[b][:].indirect(cls_h[h]))
-            for h in range(HALVES):
-                nc.vector.tensor_copy(b_picked[:, half[h]], b_raw[b][:].indirect(cls_h[h]))
-            for h in range(HALVES):
-                scaler = nc.vector if (b, h) == (BLOCKS - 1, 0) else nc.gpsimd
-                scaler.tensor_tensor(scaled[:, half[h]], y[b, h][:], g_picked[:, half[h]], MULT)
-            adder = nc.vector if b == BLOCKS - 1 else nc.gpsimd
-            for h in range(HALVES):
-                adder.tensor_tensor(result[:, half[h]], b_picked[:, half[h]], scaled[:, half[h]], ADD)
-                nc.sync.dma_start(out[b * P : (b + 1) * P, half[h]], result[:, half[h]])
+                result = keep.tile([P, H], F32, name="result%d_%d" % (b, h))
+                nc.vector.tensor_tensor(result[:], b_raw[b][:].indirect(cls_h[h]), scaled[h][:], ADD)
+                nc.sync.dma_start(out[b * P : (b + 1) * P, half[h]], result[:])

@@ -35,7 +35,10 @@ def tile_picked_cbn_none_e_kernel(tc, xT, w1, gamma, beta, offs, cls, out):
         cls_t = keep.tile([P, LIST_COLS], U16, name="cls_t")
         x_rows = xT.rearrange("(g p t) c -> g p t c", p=P, t=PACK)
         w_rows = w1.rearrange("(g p t) n -> g p t n", p=P, t=PACK)
-        w_raw = [keep.tile([P, PACK, N], F32, name="w_raw%d" % g) for g in range(PASSES)]
+        w_raw = {}
+        for b in range(BLOCKS):
+            for g in range(PASSES):
+                w_raw[g, b] = keep.tile([P, PACK, P], F32, name="w_raw%d_%d" % (g, b))
         g_raw = [keep.tile([P, U], F32, name="g_raw%d" % b) for b in range(BLOCKS)]
         b_raw = [keep.tile([P, U], F32, name="b_raw%d" % b) for b in range(BLOCKS)]
 
@@ -49,10 +52,14 @@ def tile_picked_cbn_none_e_kernel(tc, xT, w1, gamma, beta, offs, cls, out):
             if (g, t0) == (0, 0):
                 nc.sync.dma_start(offs_t[:], offs)
                 nc.sync.dma_start(cls_t[:], cls)
-        for g in range(PASSES):
-            nc.sync.dma_start(w_raw[g][:], w_rows[g])
         for b in range(BLOCKS):
+            if b == 0:
+                for g in range(PASSES):
+                    nc.sync.dma_start(w_raw[g, 0][:], w_rows[g, :, :, 0:P])
             nc.sync.dma_start(g_raw[b][:], gamma[b * P : (b + 1) * P, :])
+            if b == 0:
+                for g in range(PASSES):
+                    nc.sync.dma_start(w_raw[g, 1][:], w_rows[g, :, :, P : 2 * P])
             nc.sync.dma_start(b_raw[b][:], beta[b * P : (b + 1) * P, :])
 
         half = [slice(h * H, (h + 1) * H) for h in range(HALVES)]
@@ -89,52 +96,54 @@ def tile_picked_cbn_none_e_kernel(tc, xT, w1, gamma, beta, offs, cls, out):
                 x_bf[h][:].rearrange("p s t -> p (s t)"),
             )
 
-        w_codes = {}
-        w_scales = {}
-        for g in range(PASSES):
-            for b in range(BLOCKS):
-                w_bf = keep.tile([P, P, PACK], BF16, name="w_bf%d_%d" % (g, b), align_bytes=64)
-                woven = w_bf[:].rearrange("p (c i) t -> p c t i", i=4)
-                rows = w_raw[g][:, :, b * P : (b + 1) * P].rearrange("p t (c i) -> p c t i", i=4)
-                if (g, b) == (PASSES - 1, 0):
-                    nc.vector.tensor_copy(woven, rows)
-                else:
-                    nc.scalar.copy(woven, rows)
-                w_codes[g, b] = keep.tile([P, P], U32, name="w_codes%d_%d" % (g, b), align_bytes=64)
-                w_scales[g, b] = keep.tile([P, P], U8, name="w_scales%d_%d" % (g, b), align_bytes=64)
-                nc.vector.quantize_mx(
-                    w_codes[g, b][:].bitcast(FP8X4), w_scales[g, b][:], w_bf[:].rearrange("p n t -> p (n t)")
-                )
-
-        g_picked = [keep.tile([P, Q], F32, name="g_picked%d" % q, tag="g_picked%d" % q) for q in range(2)]
-        for q in range(2):
-            nc.vector.tensor_copy(g_picked[q][:], g_raw[0][:].indirect(cls_t[:, q * Q // 16 : (q + 1) * Q // 16]))
-
         for b in range(BLOCKS):
+            w_bf = keep.tile([P, PASSES, P, PACK], BF16, name="w_bf%d" % b, align_bytes=64)
+            w_codes = keep.tile([P, PASSES * P], U32, name="w_codes%d" % b, align_bytes=64)
+            w_scales = keep.tile([P, PASSES * P], U8, name="w_scales%d" % b, align_bytes=64)
+            for g in range(PASSES):
+                nc.scalar.copy(
+                    w_bf[:, g].rearrange("p (c i) t -> p c t i", i=4),
+                    w_raw[g, b][:].rearrange("p t (c i) -> p c t i", i=4),
+                )
+                if b == 0:
+                    nc.vector.quantize_mx(
+                        w_codes[:, g * P : (g + 1) * P].bitcast(FP8X4),
+                        w_scales[:, g * P : (g + 1) * P],
+                        w_bf[:, g].rearrange("p n t -> p (n t)"),
+                    )
+            if b == 1:
+                nc.vector.quantize_mx(
+                    w_codes[:].bitcast(FP8X4), w_scales[:], w_bf[:].rearrange("p g n t -> p (g n t)")
+                )
+            g_picked = []
+            if b == 0:
+                for h in range(HALVES):
+                    g_picked.append(keep.tile([P, H], F32, name="g_picked%d" % h))
+                    nc.vector.tensor_copy(g_picked[h][:], g_raw[b][:].indirect(cls_h[h]))
             scaled = []
             for h in range(HALVES):
-                acc = psum.tile([P, H], F32, name="acc%d_%d" % (b, h), tag="acc%d" % h)
+                acc = psum.tile([P, H], F32, name="acc%d_%d" % (b, h))
                 for g in range(PASSES):
                     nc.tensor.matmul_mx(
                         out=acc[:],
-                        lhsT=w_codes[g, b][:].bitcast(FP8X4),
-                        lhsT_scale=w_scales[g, b][:],
+                        lhsT=w_codes[:, g * P : (g + 1) * P].bitcast(FP8X4),
+                        lhsT_scale=w_scales[:, g * P : (g + 1) * P],
                         rhs=x_codes[g][:, half[h]].bitcast(FP8X4),
                         rhs_scale=x_scales[g][:, half[h]],
                         start=(g == 0),
                         stop=(g == PASSES - 1),
                     )
-                if (b, h) == (0, 0):
-                    scaled.append(keep.tile([P, H], F32, name="scaled0_0"))
-                    for q in range(2):
-                        part = slice(q * Q, (q + 1) * Q)
-                        nc.vector.tensor_tensor(scaled[h][:, part], acc[:, part], g_picked[q][:], MULT)
+                scaled.append(keep.tile([P, H], F32, name="scaled%d_%d" % (b, h)))
+                if b == 0:
+                    nc.vector.tensor_tensor(scaled[h][:], acc[:], g_picked[h][:], MULT)
                 else:
-                    scaled.append(keep.tile([P, H], F32, name="scaled%d_%d" % (b, h)))
                     y = keep.tile([P, H], F32, name="y%d_%d" % (b, h))
                     nc.scalar.copy(y[:], acc[:])
                     nc.vector.tensor_tensor(scaled[h][:], g_raw[b][:].indirect(cls_h[h]), y[:], MULT)
+            result = keep.tile([P, S], F32, name="result%d" % b)
             for h in range(HALVES):
-                result = keep.tile([P, H], F32, name="result%d_%d" % (b, h))
-                nc.vector.tensor_tensor(result[:], b_raw[b][:].indirect(cls_h[h]), scaled[h][:], ADD)
-                nc.sync.dma_start(out[b * P : (b + 1) * P, half[h]], result[:])
+                nc.vector.tensor_tensor(result[:, half[h]], b_raw[b][:].indirect(cls_h[h]), scaled[h][:], ADD)
+                if b == BLOCKS - 1:
+                    nc.sync.dma_start(out[b * P : (b + 1) * P, half[h]], result[:, half[h]])
+            if b < BLOCKS - 1:
+                nc.sync.dma_start(out[b * P : (b + 1) * P, :], result[:])

@@ -22,7 +22,6 @@ BLOCKS = N // P
 LIST_COLS = S // 16
 HALVES = 2
 H = S // HALVES
-Q = H // 2
 
 
 def tile_picked_cbn_none_e_kernel(tc, xT, w1, gamma, beta, offs, cls, out):
@@ -78,15 +77,23 @@ def tile_picked_cbn_none_e_kernel(tc, xT, w1, gamma, beta, offs, cls, out):
         x_codes = []
         x_scales = []
         x_bf = [keep.tile([P, H, PACK], BF16, name="x_bf_last%d" % h, align_bytes=64) for h in range(HALVES)]
-        for t in range(PACK):
+        early = [keep.tile([P, PACK - 1, H], F32, name="early%d" % h) for h in range(HALVES)]
+        for t in range(PACK - 1):
             for h in range(HALVES):
-                nc.vector.tensor_copy(x_bf[h][:, :, t], plane[1, t].indirect(offs_h[h]))
+                nc.vector.tensor_copy(early[h][:, t, :], plane[1, t].indirect(offs_h[h]))
             if t == 1:
                 x_codes.append(keep.tile([P, S], U32, name="x_codes0", tag="x_raw1_1", align_bytes=64))
                 x_scales.append(keep.tile([P, S], U8, name="x_scales0", align_bytes=64))
                 nc.vector.quantize_mx(
                     x_codes[0][:].bitcast(FP8X4), x_scales[0][:], x_bf_first[:].rearrange("p s t -> p (s t)")
                 )
+        for h in range(HALVES):
+            nc.vector.tensor_copy(
+                x_bf[h][:, :, 0 : PACK - 1].rearrange("p (c i) t -> p c t i", i=4),
+                early[h][:].rearrange("p t (c i) -> p c t i", i=4),
+            )
+        for h in range(HALVES):
+            nc.vector.tensor_copy(x_bf[h][:, :, PACK - 1], plane[1, PACK - 1].indirect(offs_h[h]))
         x_codes.append(keep.tile([P, S], U32, name="x_codes1", align_bytes=64))
         x_scales.append(keep.tile([P, S], U8, name="x_scales1", align_bytes=64))
         for h in range(HALVES):

@@ -50,11 +50,11 @@ def tile_picked_cbn_none_e_kernel(tc, xT, w1, gamma, beta, offs, cls, out):
                 plane[g, t0 + i] = x_raw[:, i * T : (i + 1) * T]
             if (g, t0) == (0, 0):
                 nc.sync.dma_start(offs_t[:], offs)
-                nc.sync.dma_start(cls_t[:], cls)
         for b in range(BLOCKS):
             if b == 0:
                 for g in range(PASSES):
                     nc.sync.dma_start(w_raw[g, 0][:], w_rows[g, :, :, 0:P])
+                nc.sync.dma_start(cls_t[:], cls)
             nc.sync.dma_start(g_raw[b][:], gamma[b * P : (b + 1) * P, :])
             if b == 0:
                 for g in range(PASSES):
@@ -112,15 +112,10 @@ def tile_picked_cbn_none_e_kernel(tc, xT, w1, gamma, beta, offs, cls, out):
                     w_bf[:, g].rearrange("p (c i) t -> p c t i", i=4),
                     w_raw[g, b][:].rearrange("p t (c i) -> p c t i", i=4),
                 )
-                if b == 0:
-                    nc.vector.quantize_mx(
-                        w_codes[:, g * P : (g + 1) * P].bitcast(FP8X4),
-                        w_scales[:, g * P : (g + 1) * P],
-                        w_bf[:, g].rearrange("p n t -> p (n t)"),
-                    )
-            if b == 1:
                 nc.vector.quantize_mx(
-                    w_codes[:].bitcast(FP8X4), w_scales[:], w_bf[:].rearrange("p g n t -> p (g n t)")
+                    w_codes[:, g * P : (g + 1) * P].bitcast(FP8X4),
+                    w_scales[:, g * P : (g + 1) * P],
+                    w_bf[:, g].rearrange("p n t -> p (n t)"),
                 )
             g_picked = []
             if b == 0:
@@ -130,15 +125,16 @@ def tile_picked_cbn_none_e_kernel(tc, xT, w1, gamma, beta, offs, cls, out):
             scaled = []
             for h in range(HALVES):
                 acc = psum.tile([P, H], F32, name="acc%d_%d" % (b, h))
-                for g in range(PASSES):
+                order = range(PASSES) if h == 0 else reversed(range(PASSES))
+                for step, g in enumerate(order):
                     nc.tensor.matmul_mx(
                         out=acc[:],
                         lhsT=w_codes[:, g * P : (g + 1) * P].bitcast(FP8X4),
                         lhsT_scale=w_scales[:, g * P : (g + 1) * P],
                         rhs=x_codes[g][:, half[h]].bitcast(FP8X4),
                         rhs_scale=x_scales[g][:, half[h]],
-                        start=(g == 0),
-                        stop=(g == PASSES - 1),
+                        start=(step == 0),
+                        stop=(step == PASSES - 1),
                     )
                 scaled.append(keep.tile([P, H], F32, name="scaled%d_%d" % (b, h)))
                 if b == 0:

@@ -37,7 +37,7 @@ def tile_picked_cbn_none_e_kernel(tc, xT, w1, gamma, beta, offs, cls, out):
         w_raw = {}
         for b in range(BLOCKS):
             for g in range(PASSES):
-                w_raw[g, b] = keep.tile([P, PACK, P], F32, name="w_raw%d_%d" % (g, b))
+                w_raw[g, b] = keep.tile([P, PACK, P], F32, name="w_raw%d_%d" % (g, b), tag="w_raw%d_%d" % (g, b))
         g_raw = [keep.tile([P, U], F32, name="g_raw%d" % b) for b in range(BLOCKS)]
         b_raw = [keep.tile([P, U], F32, name="b_raw%d" % b) for b in range(BLOCKS)]
 
@@ -103,50 +103,63 @@ def tile_picked_cbn_none_e_kernel(tc, xT, w1, gamma, beta, offs, cls, out):
                 x_bf[h][:].rearrange("p s t -> p (s t)"),
             )
 
+        w_bf = []
+        w_codes = []
+        w_scales = []
         for b in range(BLOCKS):
-            w_bf = keep.tile([P, PASSES, P, PACK], BF16, name="w_bf%d" % b, align_bytes=64)
-            w_codes = keep.tile([P, PASSES * P], U32, name="w_codes%d" % b, align_bytes=64)
-            w_scales = keep.tile([P, PASSES * P], U8, name="w_scales%d" % b, align_bytes=64)
-            for g in range(PASSES):
-                nc.scalar.copy(
-                    w_bf[:, g].rearrange("p (c i) t -> p c t i", i=4),
-                    w_raw[g, b][:].rearrange("p t (c i) -> p c t i", i=4),
+            w_bf.append(keep.tile([P, PASSES, P, PACK], BF16, name="w_bf%d" % b, align_bytes=64))
+            w_codes.append(keep.tile([P, PASSES * P], U32, name="w_codes%d" % b, align_bytes=64))
+            w_scales.append(keep.tile([P, PASSES * P], U8, name="w_scales%d" % b, align_bytes=64))
+
+        def quantise_w(g, b):
+            nc.scalar.copy(
+                w_bf[b][:, g].rearrange("p (c i) t -> p c t i", i=4),
+                w_raw[g, b][:].rearrange("p t (c i) -> p c t i", i=4),
+            )
+            nc.vector.quantize_mx(
+                w_codes[b][:, g * P : (g + 1) * P].bitcast(FP8X4),
+                w_scales[b][:, g * P : (g + 1) * P],
+                w_bf[b][:, g].rearrange("p n t -> p (n t)"),
+            )
+
+        def sums(b, h, order):
+            acc = psum.tile([P, H], F32, name="acc%d_%d" % (b, h))
+            for step, g in enumerate(order):
+                nc.tensor.matmul_mx(
+                    out=acc[:],
+                    lhsT=w_codes[b][:, g * P : (g + 1) * P].bitcast(FP8X4),
+                    lhsT_scale=w_scales[b][:, g * P : (g + 1) * P],
+                    rhs=x_codes[g][:, half[h]].bitcast(FP8X4),
+                    rhs_scale=x_scales[g][:, half[h]],
+                    start=(step == 0),
+                    stop=(step == PASSES - 1),
                 )
-                nc.vector.quantize_mx(
-                    w_codes[:, g * P : (g + 1) * P].bitcast(FP8X4),
-                    w_scales[:, g * P : (g + 1) * P],
-                    w_bf[:, g].rearrange("p n t -> p (n t)"),
-                )
-            g_picked = []
-            if b == 0:
-                for h in range(HALVES):
-                    g_picked.append(keep.tile([P, H], F32, name="g_picked%d" % h))
-                    nc.vector.tensor_copy(g_picked[h][:], g_raw[b][:].indirect(cls_h[h]))
-            scaled = []
-            for h in range(HALVES):
-                acc = psum.tile([P, H], F32, name="acc%d_%d" % (b, h))
-                order = range(PASSES) if h == 0 else reversed(range(PASSES))
-                for step, g in enumerate(order):
-                    nc.tensor.matmul_mx(
-                        out=acc[:],
-                        lhsT=w_codes[:, g * P : (g + 1) * P].bitcast(FP8X4),
-                        lhsT_scale=w_scales[:, g * P : (g + 1) * P],
-                        rhs=x_codes[g][:, half[h]].bitcast(FP8X4),
-                        rhs_scale=x_scales[g][:, half[h]],
-                        start=(step == 0),
-                        stop=(step == PASSES - 1),
-                    )
-                scaled.append(keep.tile([P, H], F32, name="scaled%d_%d" % (b, h)))
-                if b == 0:
-                    nc.vector.tensor_tensor(scaled[h][:], acc[:], g_picked[h][:], MULT)
-                else:
-                    y = keep.tile([P, H], F32, name="y%d_%d" % (b, h))
-                    nc.scalar.copy(y[:], acc[:])
-                    nc.vector.tensor_tensor(scaled[h][:], g_raw[b][:].indirect(cls_h[h]), y[:], MULT)
-            result = keep.tile([P, S], F32, name="result%d" % b)
-            for h in range(HALVES):
-                nc.vector.tensor_tensor(result[:, half[h]], b_raw[b][:].indirect(cls_h[h]), scaled[h][:], ADD)
-                if b == BLOCKS - 1:
-                    nc.sync.dma_start(out[b * P : (b + 1) * P, half[h]], result[:, half[h]])
-            if b < BLOCKS - 1:
-                nc.sync.dma_start(out[b * P : (b + 1) * P, :], result[:])
+            return acc
+
+        quantise_w(0, 0)
+        quantise_w(1, 0)
+        g_picked = []
+        for h in range(HALVES):
+            g_picked.append(keep.tile([P, H], F32, name="g_picked%d" % h))
+            nc.vector.tensor_copy(g_picked[h][:], g_raw[0][:].indirect(cls_h[h]))
+        first_sums = [sums(0, 0, (0, 1)), sums(0, 1, (1, 0))]
+        quantise_w(0, 1)
+        scaled0 = keep.tile([P, S], F32, name="scaled0", tag="w_raw0_1")
+        for h in range(HALVES):
+            nc.vector.tensor_tensor(scaled0[:, half[h]], first_sums[h][:], g_picked[h][:], MULT)
+        quantise_w(1, 1)
+        result0 = keep.tile([P, S], F32, name="result0")
+        nc.vector.tensor_tensor(result0[:], b_raw[0][:].indirect(cls_t[:]), scaled0[:], ADD)
+        nc.sync.dma_start(out[0:P, :], result0[:])
+
+        scaled1 = []
+        for h in range(HALVES):
+            acc = sums(1, h, (0, 1))
+            y = keep.tile([P, H], F32, name="y%d" % h)
+            nc.scalar.copy(y[:], acc[:])
+            scaled1.append(keep.tile([P, H], F32, name="scaled1_%d" % h))
+            nc.vector.tensor_tensor(scaled1[h][:], g_raw[1][:].indirect(cls_h[h]), y[:], MULT)
+        for h in range(HALVES):
+            result1 = keep.tile([P, H], F32, name="result1_%d" % h)
+            nc.vector.tensor_tensor(result1[:], b_raw[1][:].indirect(cls_h[h]), scaled1[h][:], ADD)
+            nc.sync.dma_start(out[P : 2 * P, half[h]], result1[:])

@@ -22,6 +22,11 @@ BLOCKS = N // P
 LIST_COLS = S // 16
 HALVES = 2
 H = S // HALVES
+Q = H // 2
+
+
+def entries(list_tile, part):
+    return list_tile[:, part.start // 16 : part.stop // 16]
 
 
 def tile_picked_cbn_none_e_kernel(tc, xT, w1, gamma, beta, offs, cls, out):
@@ -152,14 +157,16 @@ def tile_picked_cbn_none_e_kernel(tc, xT, w1, gamma, beta, offs, cls, out):
         nc.vector.tensor_tensor(result0[:], b_raw[0][:].indirect(cls_t[:]), scaled0[:], ADD)
         nc.sync.dma_start(out[0:P, :], result0[:])
 
-        scaled1 = []
+        scaled1 = keep.tile([P, S], F32, name="scaled1")
         for h in range(HALVES):
             acc = sums(1, h, (0, 1))
-            y = keep.tile([P, H], F32, name="y%d" % h)
-            nc.scalar.copy(y[:], acc[:])
-            scaled1.append(keep.tile([P, H], F32, name="scaled1_%d" % h))
-            nc.vector.tensor_tensor(scaled1[h][:], g_raw[1][:].indirect(cls_h[h]), y[:], MULT)
-        for h in range(HALVES):
-            result1 = keep.tile([P, H], F32, name="result1_%d" % h)
-            nc.vector.tensor_tensor(result1[:], b_raw[1][:].indirect(cls_h[h]), scaled1[h][:], ADD)
-            nc.sync.dma_start(out[P : 2 * P, half[h]], result1[:])
+            for lo, hi in ((0, Q), (Q, H)) if h == 0 else ((0, H),):
+                part = slice(h * H + lo, h * H + hi)
+                y = keep.tile([P, hi - lo], F32, name="y%d" % part.start)
+                nc.scalar.copy(y[:], acc[:, lo:hi])
+                nc.vector.tensor_tensor(scaled1[:, part], g_raw[1][:].indirect(entries(cls_t, part)), y[:], MULT)
+        for lo, hi in ((0, H), (H, S - Q), (S - Q, S)):
+            part = slice(lo, hi)
+            result1 = keep.tile([P, hi - lo], F32, name="result1_%d" % lo)
+            nc.vector.tensor_tensor(result1[:], b_raw[1][:].indirect(entries(cls_t, part)), scaled1[:, part], ADD)
+            nc.sync.dma_start(out[P : 2 * P, part], result1[:])

@@ -42,14 +42,14 @@ def tile_picked_cbn_none_e_kernel(tc, xT, w1, gamma, beta, offs, cls, out):
         w_raw = {}
         for b in range(BLOCKS):
             for g in range(PASSES):
-                w_raw[g, b] = keep.tile([P, PACK, P], F32, name="w_raw%d_%d" % (g, b), tag="w_raw%d_%d" % (g, b))
-        g_raw = [keep.tile([P, U], F32, name="g_raw%d" % b) for b in range(BLOCKS)]
-        b_raw = [keep.tile([P, U], F32, name="b_raw%d" % b) for b in range(BLOCKS)]
+                w_raw[g, b] = keep.tile([P, PACK, P], F32, name="w_raw%d_%d" % (g, b), tag="w_raw%d_%d" % (g, b), align_bytes=256)
+        g_raw = [keep.tile([P, U], F32, name="g_raw%d" % b, align_bytes=256) for b in range(BLOCKS)]
+        b_raw = [keep.tile([P, U], F32, name="b_raw%d" % b, align_bytes=256) for b in range(BLOCKS)]
 
         loads = [(0, 0, 2), (0, 2, 2), (1, 0, 1), (1, 1, 1), (1, 2, 1), (1, 3, 1)]
         plane = {}
         for g, t0, rows in loads:
-            x_raw = keep.tile([P, rows * T], F32, name="x_raw%d_%d" % (g, t0), tag="x_raw%d_%d" % (g, t0), align_bytes=64)
+            x_raw = keep.tile([P, rows * T], F32, name="x_raw%d_%d" % (g, t0), tag="x_raw%d_%d" % (g, t0), align_bytes=256)
             nc.sync.dma_start(x_raw[:], x_rows[g, :, t0 : t0 + rows, :].rearrange("p t c -> p (t c)"))
             for i in range(rows):
                 plane[g, t0 + i] = x_raw[:, i * T : (i + 1) * T]
@@ -73,7 +73,7 @@ def tile_picked_cbn_none_e_kernel(tc, xT, w1, gamma, beta, offs, cls, out):
         x_picked = keep.tile([P, PACK, S], F32, name="x_picked")
         for t in range(PACK):
             nc.vector.tensor_copy(x_picked[:, t, :], plane[0, t].indirect(offs_t[:]))
-        x_bf_first = keep.tile([P, S, PACK], BF16, name="x_bf_first", align_bytes=64)
+        x_bf_first = keep.tile([P, S, PACK], BF16, name="x_bf_first", align_bytes=256)
         nc.scalar.copy(
             x_bf_first[:].rearrange("p (c i) t -> p c t i", i=4),
             x_picked[:].rearrange("p t (c i) -> p c t i", i=4),
@@ -81,14 +81,14 @@ def tile_picked_cbn_none_e_kernel(tc, xT, w1, gamma, beta, offs, cls, out):
 
         x_codes = []
         x_scales = []
-        x_bf = [keep.tile([P, H, PACK], BF16, name="x_bf_last%d" % h, align_bytes=64) for h in range(HALVES)]
+        x_bf = [keep.tile([P, H, PACK], BF16, name="x_bf_last%d" % h, align_bytes=256) for h in range(HALVES)]
         early = [keep.tile([P, PACK - 1, H], F32, name="early%d" % h) for h in range(HALVES)]
         for t in range(PACK - 1):
             for h in range(HALVES):
                 nc.vector.tensor_copy(early[h][:, t, :], plane[1, t].indirect(offs_h[h]))
             if t == 1:
-                x_codes.append(keep.tile([P, S], U32, name="x_codes0", tag="x_raw1_1", align_bytes=64))
-                x_scales.append(keep.tile([P, S], U8, name="x_scales0", align_bytes=64))
+                x_codes.append(keep.tile([P, S], U32, name="x_codes0", tag="x_raw1_1", align_bytes=256))
+                x_scales.append(keep.tile([P, S], U8, name="x_scales0", align_bytes=256))
                 nc.vector.quantize_mx(
                     x_codes[0][:].bitcast(FP8X4), x_scales[0][:], x_bf_first[:].rearrange("p s t -> p (s t)")
                 )
@@ -99,8 +99,8 @@ def tile_picked_cbn_none_e_kernel(tc, xT, w1, gamma, beta, offs, cls, out):
             )
         for h in range(HALVES):
             nc.vector.tensor_copy(x_bf[h][:, :, PACK - 1], plane[1, PACK - 1].indirect(offs_h[h]))
-        x_codes.append(keep.tile([P, S], U32, name="x_codes1", align_bytes=64))
-        x_scales.append(keep.tile([P, S], U8, name="x_scales1", align_bytes=64))
+        x_codes.append(keep.tile([P, S], U32, name="x_codes1", align_bytes=256))
+        x_scales.append(keep.tile([P, S], U8, name="x_scales1", align_bytes=256))
         for h in range(HALVES):
             nc.vector.quantize_mx(
                 x_codes[1][:, half[h]].bitcast(FP8X4),
@@ -112,9 +112,9 @@ def tile_picked_cbn_none_e_kernel(tc, xT, w1, gamma, beta, offs, cls, out):
         w_codes = []
         w_scales = []
         for b in range(BLOCKS):
-            w_bf.append(keep.tile([P, PASSES, P, PACK], BF16, name="w_bf%d" % b, align_bytes=64))
-            w_codes.append(keep.tile([P, PASSES * P], U32, name="w_codes%d" % b, align_bytes=64))
-            w_scales.append(keep.tile([P, PASSES * P], U8, name="w_scales%d" % b, align_bytes=64))
+            w_bf.append(keep.tile([P, PASSES, P, PACK], BF16, name="w_bf%d" % b, align_bytes=256))
+            w_codes.append(keep.tile([P, PASSES * P], U32, name="w_codes%d" % b, align_bytes=256))
+            w_scales.append(keep.tile([P, PASSES * P], U8, name="w_scales%d" % b, align_bytes=256))
 
         def quantise_w(g, b):
             nc.scalar.copy(
@@ -149,11 +149,11 @@ def tile_picked_cbn_none_e_kernel(tc, xT, w1, gamma, beta, offs, cls, out):
             nc.vector.tensor_copy(g_picked[h][:], g_raw[0][:].indirect(cls_h[h]))
         first_sums = [sums(0, 0, (0, 1)), sums(0, 1, (1, 0))]
         quantise_w(0, 1)
-        scaled0 = keep.tile([P, S], F32, name="scaled0", tag="w_raw0_1")
+        scaled0 = keep.tile([P, S], F32, name="scaled0", tag="w_raw0_1", align_bytes=256)
         for h in range(HALVES):
             nc.vector.tensor_tensor(scaled0[:, half[h]], first_sums[h][:], g_picked[h][:], MULT)
         quantise_w(1, 1)
-        result0 = keep.tile([P, S], F32, name="result0")
+        result0 = keep.tile([P, S], F32, name="result0", align_bytes=256)
         nc.vector.tensor_tensor(result0[:], b_raw[0][:].indirect(cls_t[:]), scaled0[:], ADD)
         nc.sync.dma_start(out[0:P, :], result0[:])
 
@@ -167,6 +167,6 @@ def tile_picked_cbn_none_e_kernel(tc, xT, w1, gamma, beta, offs, cls, out):
                 nc.vector.tensor_tensor(scaled1[:, part], g_raw[1][:].indirect(entries(cls_t, part)), y[:], MULT)
         for lo, hi in ((0, H), (H, S - Q), (S - Q, S)):
             part = slice(lo, hi)
-            result1 = keep.tile([P, hi - lo], F32, name="result1_%d" % lo)
+            result1 = keep.tile([P, hi - lo], F32, name="result1_%d" % lo, align_bytes=256)
             nc.vector.tensor_tensor(result1[:], b_raw[1][:].indirect(entries(cls_t, part)), scaled1[:, part], ADD)
             nc.sync.dma_start(out[P : 2 * P, part], result1[:])

@@ -148,13 +148,14 @@ def tile_picked_cbn_none_e_kernel(tc, xT, w1, gamma, beta, offs, cls, out):
             g_picked.append(keep.tile([P, H], F32, name="g_picked%d" % h))
             nc.vector.tensor_copy(g_picked[h][:], g_raw[0][:].indirect(cls_h[h]))
         first_sums = [sums(0, 0, (0, 1)), sums(0, 1, (1, 0))]
-        quantise_w(0, 1)
-        scaled0 = keep.tile([P, S], F32, name="scaled0", tag="w_raw0_1", align_bytes=256)
+        scaled0 = []
         for h in range(HALVES):
-            nc.vector.tensor_tensor(scaled0[:, half[h]], first_sums[h][:], g_picked[h][:], MULT)
-        quantise_w(1, 1)
+            quantise_w(h, 1)
+            scaled0.append(keep.tile([P, H], F32, name="scaled0_%d" % h, tag="w_raw%d_1" % h, align_bytes=256))
+            nc.vector.tensor_tensor(scaled0[h][:], first_sums[h][:], g_picked[h][:], MULT)
         result0 = keep.tile([P, S], F32, name="result0", align_bytes=256)
-        nc.vector.tensor_tensor(result0[:], b_raw[0][:].indirect(cls_t[:]), scaled0[:], ADD)
+        for h in range(HALVES):
+            nc.vector.tensor_tensor(result0[:, half[h]], b_raw[0][:].indirect(cls_h[h]), scaled0[h][:], ADD)
         nc.sync.dma_start(out[0:P, :], result0[:])
 
         scaled1 = keep.tile([P, S], F32, name="scaled1")

@@ -82,23 +82,17 @@ def tile_picked_cbn_none_e_kernel(tc, xT, w1, gamma, beta, offs, cls, out):
         x_codes = []
         x_scales = []
         x_bf = [keep.tile([P, H, PACK], BF16, name="x_bf_last%d" % h, align_bytes=256) for h in range(HALVES)]
-        early = [keep.tile([P, PACK - 1, H], F32, name="early%d" % h) for h in range(HALVES)]
-        for t in range(PACK - 1):
+        pair = keep.tile([P, 2, S], F32, name="pair")
+        for t in range(2):
+            nc.vector.tensor_copy(pair[:, t, :], plane[1, t].indirect(offs_t[:]))
+        x_codes.append(keep.tile([P, S], U32, name="x_codes0", tag="x_raw1_1", align_bytes=256))
+        x_scales.append(keep.tile([P, S], U8, name="x_scales0", align_bytes=256))
+        nc.vector.quantize_mx(x_codes[0][:].bitcast(FP8X4), x_scales[0][:], x_bf_first[:].rearrange("p s t -> p (s t)"))
+        for h in range(HALVES):
+            nc.scalar.copy(x_bf[h][:, :, 0:2], pair[:, :, half[h]].rearrange("p t s -> p s t"))
+        for t in range(2, PACK):
             for h in range(HALVES):
-                nc.vector.tensor_copy(early[h][:, t, :], plane[1, t].indirect(offs_h[h]))
-            if t == 1:
-                x_codes.append(keep.tile([P, S], U32, name="x_codes0", tag="x_raw1_1", align_bytes=256))
-                x_scales.append(keep.tile([P, S], U8, name="x_scales0", align_bytes=256))
-                nc.vector.quantize_mx(
-                    x_codes[0][:].bitcast(FP8X4), x_scales[0][:], x_bf_first[:].rearrange("p s t -> p (s t)")
-                )
-        for h in range(HALVES):
-            nc.vector.tensor_copy(
-                x_bf[h][:, :, 0 : PACK - 1].rearrange("p (c i) t -> p c t i", i=4),
-                early[h][:].rearrange("p t (c i) -> p c t i", i=4),
-            )
-        for h in range(HALVES):
-            nc.vector.tensor_copy(x_bf[h][:, :, PACK - 1], plane[1, PACK - 1].indirect(offs_h[h]))
+                nc.vector.tensor_copy(x_bf[h][:, :, t], plane[1, t].indirect(offs_h[h]))
         x_codes.append(keep.tile([P, S], U32, name="x_codes1", align_bytes=256))
         x_scales.append(keep.tile([P, S], U8, name="x_scales1", align_bytes=256))
         for h in range(HALVES):

@@ -67,7 +67,6 @@ def tile_picked_cbn_none_e_kernel(tc, xT, w1, gamma, beta, offs, cls, out):
             nc.sync.dma_start(b_raw[b][:], beta[b * P : (b + 1) * P, :])
 
         half = [slice(h * H, (h + 1) * H) for h in range(HALVES)]
-        offs_h = [offs_t[:, h * H // 16 : (h + 1) * H // 16] for h in range(HALVES)]
         cls_h = [cls_t[:, h * H // 16 : (h + 1) * H // 16] for h in range(HALVES)]
 
         x_picked = keep.tile([P, PACK, S], F32, name="x_picked")
@@ -81,26 +80,16 @@ def tile_picked_cbn_none_e_kernel(tc, xT, w1, gamma, beta, offs, cls, out):
 
         x_codes = []
         x_scales = []
-        x_bf = [keep.tile([P, H, PACK], BF16, name="x_bf_last%d" % h, align_bytes=256) for h in range(HALVES)]
+        x_bf = keep.tile([P, S, PACK], BF16, name="x_bf_last", align_bytes=256)
         pair = keep.tile([P, 2, S], F32, name="pair")
         for t in range(2):
             nc.vector.tensor_copy(pair[:, t, :], plane[1, t].indirect(offs_t[:]))
         x_codes.append(keep.tile([P, S], U32, name="x_codes0", tag="x_raw1_1", align_bytes=256))
         x_scales.append(keep.tile([P, S], U8, name="x_scales0", align_bytes=256))
         nc.vector.quantize_mx(x_codes[0][:].bitcast(FP8X4), x_scales[0][:], x_bf_first[:].rearrange("p s t -> p (s t)"))
-        for h in range(HALVES):
-            nc.scalar.copy(x_bf[h][:, :, 0:2], pair[:, :, half[h]].rearrange("p t s -> p s t"))
+        nc.scalar.copy(x_bf[:, :, 0:2], pair[:].rearrange("p t s -> p s t"))
         for t in range(2, PACK):
-            for h in range(HALVES):
-                nc.vector.tensor_copy(x_bf[h][:, :, t], plane[1, t].indirect(offs_h[h]))
-        x_codes.append(keep.tile([P, S], U32, name="x_codes1", align_bytes=256))
-        x_scales.append(keep.tile([P, S], U8, name="x_scales1", align_bytes=256))
-        for h in range(HALVES):
-            nc.vector.quantize_mx(
-                x_codes[1][:, half[h]].bitcast(FP8X4),
-                x_scales[1][:, half[h]],
-                x_bf[h][:].rearrange("p s t -> p (s t)"),
-            )
+            nc.vector.tensor_copy(x_bf[:, :, t], plane[1, t].indirect(offs_t[:]))
 
         w_bf = []
         w_codes = []
@@ -136,12 +125,15 @@ def tile_picked_cbn_none_e_kernel(tc, xT, w1, gamma, beta, offs, cls, out):
             return acc
 
         quantise_w(0, 0)
+        x_codes.append(keep.tile([P, S], U32, name="x_codes1", tag="w_raw0_0", align_bytes=256))
+        x_scales.append(keep.tile([P, S], U8, name="x_scales1", align_bytes=256))
+        nc.vector.quantize_mx(x_codes[1][:].bitcast(FP8X4), x_scales[1][:], x_bf[:].rearrange("p s t -> p (s t)"))
         quantise_w(1, 0)
         g_picked = []
         for h in range(HALVES):
             g_picked.append(keep.tile([P, H], F32, name="g_picked%d" % h))
             nc.vector.tensor_copy(g_picked[h][:], g_raw[0][:].indirect(cls_h[h]))
-        first_sums = [sums(0, 0, (0, 1)), sums(0, 1, (1, 0))]
+        first_sums = [sums(0, h, (0, 1)) for h in range(HALVES)]
         scaled0 = []
         for h in range(HALVES):
             quantise_w(h, 1)
@@ -155,11 +147,9 @@ def tile_picked_cbn_none_e_kernel(tc, xT, w1, gamma, beta, offs, cls, out):
         scaled1 = keep.tile([P, S], F32, name="scaled1")
         for h in range(HALVES):
             acc = sums(1, h, (0, 1))
-            for lo, hi in ((0, Q), (Q, H)) if h == 0 else ((0, H),):
-                part = slice(h * H + lo, h * H + hi)
-                y = keep.tile([P, hi - lo], F32, name="y%d" % part.start)
-                nc.scalar.copy(y[:], acc[:, lo:hi])
-                nc.vector.tensor_tensor(scaled1[:, part], g_raw[1][:].indirect(entries(cls_t, part)), y[:], MULT)
+            y = keep.tile([P, H], F32, name="y%d" % h)
+            nc.scalar.copy(y[:], acc[:])
+            nc.vector.tensor_tensor(scaled1[:, half[h]], g_raw[1][:].indirect(cls_h[h]), y[:], MULT)
         for lo, hi in ((0, H), (H, S - Q), (S - Q, S)):
             part = slice(lo, hi)
             result1 = keep.tile([P, hi - lo], F32, name="result1_%d" % lo, align_bytes=256)

@@ -13,6 +13,7 @@ U8 = mybir.dt.uint8
 FP8X4 = mybir.dt.float8_e4m3fn_x4
 MULT = mybir.AluOpType.mult
 ADD = mybir.AluOpType.add
+COPY = mybir.ActivationFunctionType.Copy
 
 P = 128
 PACK = 4
@@ -22,11 +23,15 @@ BLOCKS = N // P
 LIST_COLS = S // 16
 HALVES = 2
 H = S // HALVES
-Q = H // 2
+G1_VECTOR = 192
 
 
 def entries(list_tile, part):
     return list_tile[:, part.start // 16 : part.stop // 16]
+
+
+def interleave(copy, dst, src):
+    copy(dst.rearrange("p (c i) t -> p c t i", i=4), src.rearrange("p t (c i) -> p c t i", i=4))
 
 
 def tile_picked_cbn_none_e_kernel(tc, xT, w1, gamma, beta, offs, cls, out):
@@ -35,123 +40,118 @@ def tile_picked_cbn_none_e_kernel(tc, xT, w1, gamma, beta, offs, cls, out):
         keep = ctx.enter_context(tc.tile_pool(name="keep", bufs=1))
         psum = ctx.enter_context(tc.psum_pool(name="psum", bufs=1))
 
+        def sbuf(name, shape, dtype, tag=None):
+            return keep.tile(shape, dtype, name=name, tag=tag or name, align_bytes=256)
+
+        half = [slice(h * H, (h + 1) * H) for h in range(HALVES)]
         offs_t = keep.tile([P, LIST_COLS], U16, name="offs_t")
         cls_t = keep.tile([P, LIST_COLS], U16, name="cls_t")
         x_rows = xT.rearrange("(g p t) c -> g p t c", p=P, t=PACK)
-        w_rows = w1.rearrange("(g p t) n -> g p t n", p=P, t=PACK)
-        w_raw = {}
-        for b in range(BLOCKS):
-            for g in range(PASSES):
-                w_raw[g, b] = keep.tile([P, PACK, P], F32, name="w_raw%d_%d" % (g, b), tag="w_raw%d_%d" % (g, b), align_bytes=256)
-        g_raw = [keep.tile([P, U], F32, name="g_raw%d" % b, align_bytes=256) for b in range(BLOCKS)]
-        b_raw = [keep.tile([P, U], F32, name="b_raw%d" % b, align_bytes=256) for b in range(BLOCKS)]
 
-        loads = [(0, 0, 2), (0, 2, 2), (1, 0, 1), (1, 1, 1), (1, 2, 1), (1, 3, 1)]
+        w_rows = w1.rearrange("(g p t) n -> g p t n", p=P, t=PACK)
+        w_raw = [sbuf("w_raw%d" % g, [P, PACK, N], F32) for g in range(PASSES)]
+        nc.sync.dma_start(w_raw[0][:], w_rows[0])
         plane = {}
-        for g, t0, rows in loads:
-            x_raw = keep.tile([P, rows * T], F32, name="x_raw%d_%d" % (g, t0), tag="x_raw%d_%d" % (g, t0), align_bytes=256)
+        for g, t0, rows in [(0, 0, 4), (1, 0, 2), (1, 2, 1), (1, 3, 1)]:
+            x_raw = sbuf("x_raw%d_%d" % (g, t0), [P, rows * T], F32)
             nc.sync.dma_start(x_raw[:], x_rows[g, :, t0 : t0 + rows, :].rearrange("p t c -> p (t c)"))
             for i in range(rows):
                 plane[g, t0 + i] = x_raw[:, i * T : (i + 1) * T]
-            if (g, t0) == (0, 0):
+            if g == 0:
                 nc.sync.dma_start(offs_t[:], offs)
-        for b in range(BLOCKS):
-            if b == 0:
-                for g in range(PASSES):
-                    nc.sync.dma_start(w_raw[g, 0][:], w_rows[g, :, :, 0:P])
                 nc.sync.dma_start(cls_t[:], cls)
-            nc.sync.dma_start(g_raw[b][:], gamma[b * P : (b + 1) * P, :])
-            if b == 0:
-                for g in range(PASSES):
-                    nc.sync.dma_start(w_raw[g, 1][:], w_rows[g, :, :, P : 2 * P])
-            nc.sync.dma_start(b_raw[b][:], beta[b * P : (b + 1) * P, :])
+        nc.sync.dma_start(w_raw[1][:], w_rows[1])
+        g_raw = [sbuf("g_raw%d" % b, [P, U], F32) for b in range(BLOCKS)]
+        b_raw = [sbuf("b_raw%d" % b, [P, U], F32) for b in range(BLOCKS)]
+        for raw, table in ((g_raw, gamma), (b_raw, beta)):
+            for b in range(BLOCKS):
+                nc.sync.dma_start(raw[b][:], table[b * P : (b + 1) * P, :])
 
-        half = [slice(h * H, (h + 1) * H) for h in range(HALVES)]
-        cls_h = [cls_t[:, h * H // 16 : (h + 1) * H // 16] for h in range(HALVES)]
-
-        x_picked = keep.tile([P, PACK, S], F32, name="x_picked")
-        for t in range(PACK):
-            nc.vector.tensor_copy(x_picked[:, t, :], plane[0, t].indirect(offs_t[:]))
-        x_bf_first = keep.tile([P, S, PACK], BF16, name="x_bf_first", align_bytes=256)
-        nc.scalar.copy(
-            x_bf_first[:].rearrange("p (c i) t -> p c t i", i=4),
-            x_picked[:].rearrange("p t (c i) -> p c t i", i=4),
-        )
-
-        x_codes = []
-        x_scales = []
-        x_bf = keep.tile([P, S, PACK], BF16, name="x_bf_last", align_bytes=256)
-        pair = keep.tile([P, 2, S], F32, name="pair")
-        for t in range(2):
-            nc.vector.tensor_copy(pair[:, t, :], plane[1, t].indirect(offs_t[:]))
-        x_codes.append(keep.tile([P, S], U32, name="x_codes0", tag="x_raw1_1", align_bytes=256))
-        x_scales.append(keep.tile([P, S], U8, name="x_scales0", align_bytes=256))
-        nc.vector.quantize_mx(x_codes[0][:].bitcast(FP8X4), x_scales[0][:], x_bf_first[:].rearrange("p s t -> p (s t)"))
-        nc.scalar.copy(x_bf[:, :, 0:2], pair[:].rearrange("p t s -> p s t"))
-        for t in range(2, PACK):
-            nc.vector.tensor_copy(x_bf[:, :, t], plane[1, t].indirect(offs_t[:]))
-
-        w_bf = []
-        w_codes = []
-        w_scales = []
-        for b in range(BLOCKS):
-            w_bf.append(keep.tile([P, PASSES, P, PACK], BF16, name="w_bf%d" % b, align_bytes=256))
-            w_codes.append(keep.tile([P, PASSES * P], U32, name="w_codes%d" % b, align_bytes=256))
-            w_scales.append(keep.tile([P, PASSES * P], U8, name="w_scales%d" % b, align_bytes=256))
+        w_codes = {}
+        w_scales = {}
 
         def quantise_w(g, b):
-            nc.scalar.copy(
-                w_bf[b][:, g].rearrange("p (c i) t -> p c t i", i=4),
-                w_raw[g, b][:].rearrange("p t (c i) -> p c t i", i=4),
-            )
+            w_bf = sbuf("w_bf%d_%d" % (g, b), [P, P, PACK], BF16)
+            w_codes[g, b] = sbuf("w_codes%d_%d" % (g, b), [P, P], U32)
+            w_scales[g, b] = sbuf("w_scales%d_%d" % (g, b), [P, P], U8)
+            interleave(nc.scalar.copy, w_bf[:], w_raw[g][:, :, b * P : (b + 1) * P])
+            nc.vector.quantize_mx(w_codes[g, b][:].bitcast(FP8X4), w_scales[g, b][:], w_bf[:].rearrange("p n t -> p (n t)"))
+
+        for b in range(BLOCKS):
+            quantise_w(0, b)
+
+        x_bf = [sbuf("x_bf%d" % g, [P, S, PACK], BF16) for g in range(PASSES)]
+        x_codes = [sbuf("x_codes%d" % g, [P, S], U32) for g in range(PASSES)]
+        x_scales = [sbuf("x_scales%d" % g, [P, S], U8) for g in range(PASSES)]
+        acc = {}
+        for b in range(BLOCKS):
+            for h in range(HALVES):
+                acc[b, h] = psum.tile([P, H], F32, name="acc%d_%d" % (b, h))
+
+        def quantise_x(g, h):
             nc.vector.quantize_mx(
-                w_codes[b][:, g * P : (g + 1) * P].bitcast(FP8X4),
-                w_scales[b][:, g * P : (g + 1) * P],
-                w_bf[b][:, g].rearrange("p n t -> p (n t)"),
+                x_codes[g][:, half[h]].bitcast(FP8X4),
+                x_scales[g][:, half[h]],
+                x_bf[g][:, half[h], :].rearrange("p s t -> p (s t)"),
             )
 
-        def sums(b, h, order):
-            acc = psum.tile([P, H], F32, name="acc%d_%d" % (b, h))
-            for step, g in enumerate(order):
-                nc.tensor.matmul_mx(
-                    out=acc[:],
-                    lhsT=w_codes[b][:, g * P : (g + 1) * P].bitcast(FP8X4),
-                    lhsT_scale=w_scales[b][:, g * P : (g + 1) * P],
-                    rhs=x_codes[g][:, half[h]].bitcast(FP8X4),
-                    rhs_scale=x_scales[g][:, half[h]],
-                    start=(step == 0),
-                    stop=(step == PASSES - 1),
-                )
-            return acc
+        def multiply(g, b, h):
+            nc.tensor.matmul_mx(
+                out=acc[b, h][:],
+                lhsT=w_codes[g, b][:].bitcast(FP8X4),
+                lhsT_scale=w_scales[g, b][:],
+                rhs=x_codes[g][:, half[h]].bitcast(FP8X4),
+                rhs_scale=x_scales[g][:, half[h]],
+                start=(g == 0),
+                stop=(g == PASSES - 1),
+            )
 
-        quantise_w(0, 0)
-        x_codes.append(keep.tile([P, S], U32, name="x_codes1", tag="w_raw0_0", align_bytes=256))
-        x_scales.append(keep.tile([P, S], U8, name="x_scales1", align_bytes=256))
-        nc.vector.quantize_mx(x_codes[1][:].bitcast(FP8X4), x_scales[1][:], x_bf[:].rearrange("p s t -> p (s t)"))
-        quantise_w(1, 0)
-        g_picked = []
+        picked = sbuf("picked", [P, PACK, S], F32)
+        for t in range(2):
+            nc.vector.tensor_copy(picked[:, t, :], plane[0, t].indirect(offs_t[:]))
+            nc.scalar.activation(picked[:, 2 + t, :], plane[0, 2 + t].indirect(offs_t[:]), COPY)
+        interleave(nc.vector.tensor_copy, x_bf[0][:, half[0], :], picked[:, :, half[0]])
+        interleave(nc.scalar.copy, x_bf[0][:, half[1], :], picked[:, :, half[1]])
         for h in range(HALVES):
-            g_picked.append(keep.tile([P, H], F32, name="g_picked%d" % h))
-            nc.vector.tensor_copy(g_picked[h][:], g_raw[0][:].indirect(cls_h[h]))
-        first_sums = [sums(0, h, (0, 1)) for h in range(HALVES)]
-        scaled0 = []
-        for h in range(HALVES):
-            quantise_w(h, 1)
-            scaled0.append(keep.tile([P, H], F32, name="scaled0_%d" % h, tag="w_raw%d_1" % h, align_bytes=256))
-            nc.vector.tensor_tensor(scaled0[h][:], first_sums[h][:], g_picked[h][:], MULT)
-        result0 = keep.tile([P, S], F32, name="result0", align_bytes=256)
-        for h in range(HALVES):
-            nc.vector.tensor_tensor(result0[:, half[h]], b_raw[0][:].indirect(cls_h[h]), scaled0[h][:], ADD)
-        nc.sync.dma_start(out[0:P, :], result0[:])
+            quantise_x(0, h)
+            for b in range(BLOCKS):
+                multiply(0, b, h)
 
-        scaled1 = keep.tile([P, S], F32, name="scaled1")
+        pair = sbuf("pair", [P, 2, S], F32)
+        nc.vector.tensor_copy(pair[:, 0, :], plane[1, 0].indirect(offs_t[:]))
+        nc.scalar.activation(pair[:, 1, :], plane[1, 1].indirect(offs_t[:]), COPY)
+        nc.scalar.copy(x_bf[1][:, :, 0:2], pair[:].rearrange("p t s -> p s t"))
+        nc.vector.tensor_copy(x_bf[1][:, :, 2], plane[1, 2].indirect(offs_t[:]))
         for h in range(HALVES):
-            acc = sums(1, h, (0, 1))
-            y = keep.tile([P, H], F32, name="y%d" % h)
-            nc.scalar.copy(y[:], acc[:])
-            nc.vector.tensor_tensor(scaled1[:, half[h]], g_raw[1][:].indirect(cls_h[h]), y[:], MULT)
-        for lo, hi in ((0, H), (H, S - Q), (S - Q, S)):
-            part = slice(lo, hi)
-            result1 = keep.tile([P, hi - lo], F32, name="result1_%d" % lo, align_bytes=256)
-            nc.vector.tensor_tensor(result1[:], b_raw[1][:].indirect(entries(cls_t, part)), scaled1[:, part], ADD)
-            nc.sync.dma_start(out[P : 2 * P, part], result1[:])
+            nc.vector.tensor_copy(x_bf[1][:, half[h], 3], plane[1, 3].indirect(entries(offs_t, half[h])))
+        for h in range(HALVES):
+            quantise_x(1, h)
+        for b in range(BLOCKS):
+            quantise_w(1, b)
+            for h in range(HALVES):
+                multiply(1, b, h)
+
+        g_picked = [sbuf("g_picked%d" % b, [P, S], F32) for b in range(BLOCKS)]
+        scaled = [sbuf("scaled%d" % b, [P, S], F32) for b in range(BLOCKS)]
+        for b, vector_share in enumerate((H, G1_VECTOR)):
+            cut = S - vector_share
+            for lo, hi in ((0, H), (H, cut)):
+                if hi > lo:
+                    nc.scalar.activation(g_picked[b][:, lo:hi], g_raw[b][:].indirect(entries(cls_t, slice(lo, hi))), COPY)
+            nc.vector.tensor_copy(g_picked[b][:, cut:S], g_raw[b][:].indirect(entries(cls_t, slice(cut, S))))
+        for b in range(BLOCKS):
+            for h in range(HALVES):
+                nc.vector.tensor_tensor(scaled[b][:, half[h]], acc[b, h][:], g_picked[b][:, half[h]], MULT)
+
+        for b in range(BLOCKS):
+            b_picked = sbuf("b_picked%d" % b, [P, H], F32)
+            nc.scalar.activation(b_picked[:], b_raw[b][:].indirect(entries(cls_t, half[1])), COPY)
+            result = sbuf("result%d" % b, [P, S], F32)
+            nc.vector.tensor_tensor(result[:, half[0]], b_raw[b][:].indirect(entries(cls_t, half[0])), scaled[b][:, half[0]], ADD)
+            if b == 1:
+                nc.sync.dma_start(out[b * P : (b + 1) * P, half[0]], result[:, half[0]])
+            nc.vector.tensor_tensor(result[:, half[1]], b_picked[:], scaled[b][:, half[1]], ADD)
+            if b == 1:
+                nc.sync.dma_start(out[b * P : (b + 1) * P, half[1]], result[:, half[1]])
+            else:
+                nc.sync.dma_start(out[b * P : (b + 1) * P, :], result[:])

@@ -23,7 +23,8 @@ BLOCKS = N // P
 LIST_COLS = S // 16
 HALVES = 2
 H = S // HALVES
-G1_VECTOR = 192
+G_SCALAR = ((128, 160), (160, 160))
+B_FUSED = (256, 288)
 
 
 def entries(list_tile, part):
@@ -50,16 +51,15 @@ def tile_picked_cbn_none_e_kernel(tc, xT, w1, gamma, beta, offs, cls, out):
 
         w_rows = w1.rearrange("(g p t) n -> g p t n", p=P, t=PACK)
         w_raw = [sbuf("w_raw%d" % g, [P, PACK, N], F32) for g in range(PASSES)]
-        nc.sync.dma_start(w_raw[0][:], w_rows[0])
+        nc.scalar.dma_start(w_raw[0][:], w_rows[0])
+        nc.sync.dma_start(offs_t[:], offs)
+        nc.sync.dma_start(cls_t[:], cls)
         plane = {}
         for g, t0, rows in [(0, 0, 4), (1, 0, 2), (1, 2, 1), (1, 3, 1)]:
             x_raw = sbuf("x_raw%d_%d" % (g, t0), [P, rows * T], F32)
             nc.sync.dma_start(x_raw[:], x_rows[g, :, t0 : t0 + rows, :].rearrange("p t c -> p (t c)"))
             for i in range(rows):
                 plane[g, t0 + i] = x_raw[:, i * T : (i + 1) * T]
-            if g == 0:
-                nc.sync.dma_start(offs_t[:], offs)
-                nc.sync.dma_start(cls_t[:], cls)
         nc.sync.dma_start(w_raw[1][:], w_rows[1])
         g_raw = [sbuf("g_raw%d" % b, [P, U], F32) for b in range(BLOCKS)]
         b_raw = [sbuf("b_raw%d" % b, [P, U], F32) for b in range(BLOCKS)]
@@ -131,27 +131,28 @@ def tile_picked_cbn_none_e_kernel(tc, xT, w1, gamma, beta, offs, cls, out):
             for h in range(HALVES):
                 multiply(1, b, h)
 
-        g_picked = [sbuf("g_picked%d" % b, [P, S], F32) for b in range(BLOCKS)]
         scaled = [sbuf("scaled%d" % b, [P, S], F32) for b in range(BLOCKS)]
-        for b, vector_share in enumerate((H, G1_VECTOR)):
-            cut = S - vector_share
-            for lo, hi in ((0, H), (H, cut)):
-                if hi > lo:
-                    nc.scalar.activation(g_picked[b][:, lo:hi], g_raw[b][:].indirect(entries(cls_t, slice(lo, hi))), COPY)
-            nc.vector.tensor_copy(g_picked[b][:, cut:S], g_raw[b][:].indirect(entries(cls_t, slice(cut, S))))
         for b in range(BLOCKS):
+            g_picked = sbuf("g_picked%d" % b, [P, S], F32)
             for h in range(HALVES):
-                nc.vector.tensor_tensor(scaled[b][:, half[h]], acc[b, h][:], g_picked[b][:, half[h]], MULT)
+                cut = h * H + G_SCALAR[b][h]
+                plain, rest = slice(h * H, cut), slice(cut, (h + 1) * H)
+                nc.scalar.activation(g_picked[:, plain], g_raw[b][:].indirect(entries(cls_t, plain)), COPY)
+                nc.vector.tensor_copy(g_picked[:, rest], g_raw[b][:].indirect(entries(cls_t, rest)))
+            for h in range(HALVES):
+                nc.vector.tensor_tensor(scaled[b][:, half[h]], acc[b, h][:], g_picked[:, half[h]], MULT)
 
-        for b in range(BLOCKS):
-            b_picked = sbuf("b_picked%d" % b, [P, H], F32)
-            nc.scalar.activation(b_picked[:], b_raw[b][:].indirect(entries(cls_t, half[1])), COPY)
+        for b, fused in enumerate(B_FUSED):
+            first, rest = slice(0, fused), slice(fused, S)
+            rows = slice(b * P, (b + 1) * P)
+            b_picked = sbuf("b_picked%d" % b, [P, S - fused], F32)
+            nc.scalar.activation(b_picked[:], b_raw[b][:].indirect(entries(cls_t, rest)), COPY)
             result = sbuf("result%d" % b, [P, S], F32)
-            nc.vector.tensor_tensor(result[:, half[0]], b_raw[b][:].indirect(entries(cls_t, half[0])), scaled[b][:, half[0]], ADD)
+            nc.vector.tensor_tensor(result[:, first], b_raw[b][:].indirect(entries(cls_t, first)), scaled[b][:, first], ADD)
             if b == 1:
-                nc.sync.dma_start(out[b * P : (b + 1) * P, half[0]], result[:, half[0]])
-            nc.vector.tensor_tensor(result[:, half[1]], b_picked[:], scaled[b][:, half[1]], ADD)
+                nc.sync.dma_start(out[rows, first], result[:, first])
+            nc.vector.tensor_tensor(result[:, rest], b_picked[:], scaled[b][:, rest], ADD)
             if b == 1:
-                nc.sync.dma_start(out[b * P : (b + 1) * P, half[1]], result[:, half[1]])
+                nc.sync.dma_start(out[rows, rest], result[:, rest])
             else:
-                nc.sync.dma_start(out[b * P : (b + 1) * P, :], result[:])
+                nc.sync.dma_start(out[rows, :], result[:])

@@ -23,7 +23,7 @@ BLOCKS = N // P
 LIST_COLS = S // 16
 HALVES = 2
 H = S // HALVES
-G_SCALAR = ((128, 160), (160, 160))
+G_SCALAR = ((192, 160), (256, 160))
 B_FUSED = (256, 288)
 
 
@@ -138,7 +138,8 @@ def tile_picked_cbn_none_e_kernel(tc, xT, w1, gamma, beta, offs, cls, out):
                 cut = h * H + G_SCALAR[b][h]
                 plain, rest = slice(h * H, cut), slice(cut, (h + 1) * H)
                 nc.scalar.activation(g_picked[:, plain], g_raw[b][:].indirect(entries(cls_t, plain)), COPY)
-                nc.vector.tensor_copy(g_picked[:, rest], g_raw[b][:].indirect(entries(cls_t, rest)))
+                if cut < rest.stop:
+                    nc.vector.tensor_copy(g_picked[:, rest], g_raw[b][:].indirect(entries(cls_t, rest)))
             for h in range(HALVES):
                 nc.vector.tensor_tensor(scaled[b][:, half[h]], acc[b, h][:], g_picked[:, half[h]], MULT)
 

@@ -23,8 +23,9 @@ BLOCKS = N // P
 LIST_COLS = S // 16
 HALVES = 2
 H = S // HALVES
-G_SCALAR = ((192, 160), (256, 160))
-B_FUSED = (256, 288)
+X_SCALAR = 128
+G_SCALAR = ((192, 192), (256, 192))
+B_FUSED = (224, 288)
 
 
 def entries(list_tile, part):
@@ -121,9 +122,13 @@ def tile_picked_cbn_none_e_kernel(tc, xT, w1, gamma, beta, offs, cls, out):
         nc.vector.tensor_copy(pair[:, 0, :], plane[1, 0].indirect(offs_t[:]))
         nc.scalar.activation(pair[:, 1, :], plane[1, 1].indirect(offs_t[:]), COPY)
         nc.scalar.copy(x_bf[1][:, :, 0:2], pair[:].rearrange("p t s -> p s t"))
-        nc.vector.tensor_copy(x_bf[1][:, :, 2], plane[1, 2].indirect(offs_t[:]))
-        for h in range(HALVES):
-            nc.vector.tensor_copy(x_bf[1][:, half[h], 3], plane[1, 3].indirect(entries(offs_t, half[h])))
+        stepped, paired = slice(0, S - X_SCALAR), slice(S - X_SCALAR, S)
+        last_pair = sbuf("last_pair", [P, 2, X_SCALAR], F32)
+        nc.vector.tensor_copy(x_bf[1][:, stepped, 2], plane[1, 2].indirect(entries(offs_t, stepped)))
+        for t in range(2):
+            nc.scalar.activation(last_pair[:, t, :], plane[1, 2 + t].indirect(entries(offs_t, paired)), COPY)
+        nc.scalar.copy(x_bf[1][:, paired, 2:4], last_pair[:].rearrange("p t s -> p s t"))
+        nc.vector.tensor_copy(x_bf[1][:, stepped, 3], plane[1, 3].indirect(entries(offs_t, stepped)))
         for h in range(HALVES):
             quantise_x(1, h)
         for b in range(BLOCKS):

@@ -23,7 +23,6 @@ BLOCKS = N // P
 LIST_COLS = S // 16
 HALVES = 2
 H = S // HALVES
-X_SCALAR = 128
 G_SCALAR = ((192, 192), (256, 192))
 B_FUSED = (224, 288)
 
@@ -82,7 +81,7 @@ def tile_picked_cbn_none_e_kernel(tc, xT, w1, gamma, beta, offs, cls, out):
             quantise_w(0, b)
 
         x_bf = [sbuf("x_bf%d" % g, [P, S, PACK], BF16) for g in range(PASSES)]
-        x_codes = [sbuf("x_codes%d" % g, [P, S], U32) for g in range(PASSES)]
+        x_codes = {0: sbuf("x_codes0", [P, S], U32)}
         x_scales = [sbuf("x_scales%d" % g, [P, S], U8) for g in range(PASSES)]
         acc = {}
         for b in range(BLOCKS):
@@ -118,17 +117,12 @@ def tile_picked_cbn_none_e_kernel(tc, xT, w1, gamma, beta, offs, cls, out):
             for b in range(BLOCKS):
                 multiply(0, b, h)
 
-        pair = sbuf("pair", [P, 2, S], F32)
-        nc.vector.tensor_copy(pair[:, 0, :], plane[1, 0].indirect(offs_t[:]))
-        nc.scalar.activation(pair[:, 1, :], plane[1, 1].indirect(offs_t[:]), COPY)
-        nc.scalar.copy(x_bf[1][:, :, 0:2], pair[:].rearrange("p t s -> p s t"))
-        stepped, paired = slice(0, S - X_SCALAR), slice(S - X_SCALAR, S)
-        last_pair = sbuf("last_pair", [P, 2, X_SCALAR], F32)
-        nc.vector.tensor_copy(x_bf[1][:, stepped, 2], plane[1, 2].indirect(entries(offs_t, stepped)))
-        for t in range(2):
-            nc.scalar.activation(last_pair[:, t, :], plane[1, 2 + t].indirect(entries(offs_t, paired)), COPY)
-        nc.scalar.copy(x_bf[1][:, paired, 2:4], last_pair[:].rearrange("p t s -> p s t"))
-        nc.vector.tensor_copy(x_bf[1][:, stepped, 3], plane[1, 3].indirect(entries(offs_t, stepped)))
+        late = sbuf("late", [P, PACK, H], F32)
+        for t in range(PACK):
+            nc.vector.tensor_copy(x_bf[1][:, half[0], t], plane[1, t].indirect(entries(offs_t, half[0])))
+            nc.scalar.activation(late[:, t, :], plane[1, t].indirect(entries(offs_t, half[1])), COPY)
+        interleave(nc.vector.tensor_copy, x_bf[1][:, half[1], :], late[:])
+        x_codes[1] = sbuf("x_codes1", [P, S], U32, "x_raw1_3")
         for h in range(HALVES):
             quantise_x(1, h)
         for b in range(BLOCKS):

@@ -23,8 +23,9 @@ BLOCKS = N // P
 LIST_COLS = S // 16
 HALVES = 2
 H = S // HALVES
-G_SCALAR = ((192, 192), (256, 192))
-B_FUSED = (224, 288)
+X_WOVEN_BY_SCALAR = 96
+G_SCALAR = ((192, 192), (256, 128))
+B_FUSED = (192, 288)
 
 
 def entries(list_tile, part):
@@ -118,10 +119,14 @@ def tile_picked_cbn_none_e_kernel(tc, xT, w1, gamma, beta, offs, cls, out):
                 multiply(0, b, h)
 
         late = sbuf("late", [P, PACK, H], F32)
+        shares = [(slice(0, X_WOVEN_BY_SCALAR), nc.scalar.copy), (slice(X_WOVEN_BY_SCALAR, H), nc.vector.tensor_copy)]
         for t in range(PACK):
             nc.vector.tensor_copy(x_bf[1][:, half[0], t], plane[1, t].indirect(entries(offs_t, half[0])))
-            nc.scalar.activation(late[:, t, :], plane[1, t].indirect(entries(offs_t, half[1])), COPY)
-        interleave(nc.vector.tensor_copy, x_bf[1][:, half[1], :], late[:])
+            for part in [part for part, copy in shares] if t == PACK - 1 else [slice(0, H)]:
+                listed = slice(H + part.start, H + part.stop)
+                nc.scalar.activation(late[:, t, part], plane[1, t].indirect(entries(offs_t, listed)), COPY)
+        for part, copy in shares:
+            interleave(copy, x_bf[1][:, H + part.start : H + part.stop, :], late[:, :, part])
         x_codes[1] = sbuf("x_codes1", [P, S], U32, "x_raw1_3")
         for h in range(HALVES):
             quantise_x(1, h)

@@ -56,7 +56,7 @@ def tile_picked_cbn_none_e_kernel(tc, xT, w1, gamma, beta, offs, cls, out):
         nc.sync.dma_start(offs_t[:], offs)
         nc.sync.dma_start(cls_t[:], cls)
         plane = {}
-        for g, t0, rows in [(0, 0, 4), (1, 0, 2), (1, 2, 1), (1, 3, 1)]:
+        for g, t0, rows in [(0, 0, 4), (1, 0, 3), (1, 3, 1)]:
             x_raw = sbuf("x_raw%d_%d" % (g, t0), [P, rows * T], F32)
             nc.sync.dma_start(x_raw[:], x_rows[g, :, t0 : t0 + rows, :].rearrange("p t c -> p (t c)"))
             for i in range(rows):
@@ -154,10 +154,6 @@ def tile_picked_cbn_none_e_kernel(tc, xT, w1, gamma, beta, offs, cls, out):
             nc.scalar.activation(b_picked[:], b_raw[b][:].indirect(entries(cls_t, rest)), COPY)
             result = sbuf("result%d" % b, [P, S], F32)
             nc.vector.tensor_tensor(result[:, first], b_raw[b][:].indirect(entries(cls_t, first)), scaled[b][:, first], ADD)
-            if b == 1:
-                nc.sync.dma_start(out[rows, first], result[:, first])
+            nc.sync.dma_start(out[rows, first], result[:, first])
             nc.vector.tensor_tensor(result[:, rest], b_picked[:], scaled[b][:, rest], ADD)
-            if b == 1:
-                nc.sync.dma_start(out[rows, rest], result[:, rest])
-            else:
-                nc.sync.dma_start(out[rows, :], result[:])
+            nc.sync.dma_start(out[rows, rest], result[:, rest])

@@ -25,7 +25,7 @@ HALVES = 2
 H = S // HALVES
 X_WOVEN_BY_SCALAR = 96
 G_SCALAR = ((192, 192), (256, 128))
-B_FUSED = (192, 288)
+B_FUSED = ((192,), (192, 320))
 
 
 def entries(list_tile, part):
@@ -147,13 +147,17 @@ def tile_picked_cbn_none_e_kernel(tc, xT, w1, gamma, beta, offs, cls, out):
             for h in range(HALVES):
                 nc.vector.tensor_tensor(scaled[b][:, half[h]], acc[b, h][:], g_picked[:, half[h]], MULT)
 
-        for b, fused in enumerate(B_FUSED):
-            first, rest = slice(0, fused), slice(fused, S)
+        for b, cuts in enumerate(B_FUSED):
+            fused = [slice(lo, hi) for lo, hi in zip((0,) + cuts, cuts)]
+            rest = slice(cuts[-1], S)
             rows = slice(b * P, (b + 1) * P)
-            b_picked = sbuf("b_picked%d" % b, [P, S - fused], F32)
+            b_picked = sbuf("b_picked%d" % b, [P, S - rest.start], F32)
             nc.scalar.activation(b_picked[:], b_raw[b][:].indirect(entries(cls_t, rest)), COPY)
             result = sbuf("result%d" % b, [P, S], F32)
-            nc.vector.tensor_tensor(result[:, first], b_raw[b][:].indirect(entries(cls_t, first)), scaled[b][:, first], ADD)
-            nc.sync.dma_start(out[rows, first], result[:, first])
+            for part in fused:
+                nc.vector.tensor_tensor(result[:, part], b_raw[b][:].indirect(entries(cls_t, part)), scaled[b][:, part], ADD)
+                if b == BLOCKS - 1:
+                    nc.sync.dma_start(out[rows, part], result[:, part])
             nc.vector.tensor_tensor(result[:, rest], b_picked[:], scaled[b][:, rest], ADD)
-            nc.sync.dma_start(out[rows, rest], result[:, rest])
+            stored = rest if b == BLOCKS - 1 else slice(0, S)
+            nc.sync.dma_start(out[rows, stored], result[:, stored])

@@ -120,8 +120,12 @@ def tile_picked_cbn_none_e_kernel(tc, xT, w1, gamma, beta, offs, cls, out):
 
         late = sbuf("late", [P, PACK, H], F32)
         shares = [(slice(0, X_WOVEN_BY_SCALAR), nc.scalar.copy), (slice(X_WOVEN_BY_SCALAR, H), nc.vector.tensor_copy)]
+        pair = sbuf("pair", [P, 2, H], F32)
         for t in range(PACK):
-            nc.vector.tensor_copy(x_bf[1][:, half[0], t], plane[1, t].indirect(entries(offs_t, half[0])))
+            gathered = pair[:, t, :] if t < 2 else x_bf[1][:, half[0], t]
+            nc.vector.tensor_copy(gathered, plane[1, t].indirect(entries(offs_t, half[0])))
+            if t == 2:
+                nc.vector.tensor_copy(x_bf[1][:, half[0], 0:2], pair[:].rearrange("p t s -> p s t"))
             for part in [part for part, copy in shares] if t == PACK - 1 else [slice(0, H)]:
                 listed = slice(H + part.start, H + part.stop)
                 nc.scalar.activation(late[:, t, part], plane[1, t].indirect(entries(offs_t, listed)), COPY)

@@ -23,9 +23,9 @@ BLOCKS = N // P
 LIST_COLS = S // 16
 HALVES = 2
 H = S // HALVES
-X_WOVEN_BY_SCALAR = 96
+X_WOVEN_BY_SCALAR = 128
 G_SCALAR = ((192, 192), (256, 128))
-B_FUSED = ((192,), (192, 320))
+B_FUSED = ((224,), (192, 320))
 
 
 def entries(list_tile, part):

from contextlib import ExitStack

import concourse.mybir as mybir

K, T, S, N, U = 1024, 2048, 512, 256, 1024
FLOPS = 2 * K * N * S

F32 = mybir.dt.float32
BF16 = mybir.dt.bfloat16
U32 = mybir.dt.uint32
U16 = mybir.dt.uint16
U8 = mybir.dt.uint8
FP8X4 = mybir.dt.float8_e4m3fn_x4
MULT = mybir.AluOpType.mult
ADD = mybir.AluOpType.add
COPY = mybir.ActivationFunctionType.Copy

P = 128
PACK = 4
K_PASS = P * PACK
PASSES = K // K_PASS
BLOCKS = N // P
LIST_COLS = S // 16
HALVES = 2
H = S // HALVES
X_WOVEN_BY_SCALAR = 128
G_SCALAR = ((192, 192), (256, 128))
B_FUSED = ((224,), (192, 320))


def entries(list_tile, part):
    return list_tile[:, part.start // 16 : part.stop // 16]


def interleave(copy, dst, src):
    copy(dst.rearrange("p (c i) t -> p c t i", i=4), src.rearrange("p t (c i) -> p c t i", i=4))


def tile_picked_cbn_none_e_kernel(tc, xT, w1, gamma, beta, offs, cls, out):
    nc = tc.nc
    with ExitStack() as ctx:
        keep = ctx.enter_context(tc.tile_pool(name="keep", bufs=1))
        psum = ctx.enter_context(tc.psum_pool(name="psum", bufs=1))

        def sbuf(name, shape, dtype, tag=None):
            return keep.tile(shape, dtype, name=name, tag=tag or name, align_bytes=256)

        half = [slice(h * H, (h + 1) * H) for h in range(HALVES)]
        offs_t = keep.tile([P, LIST_COLS], U16, name="offs_t")
        cls_t = keep.tile([P, LIST_COLS], U16, name="cls_t")
        x_rows = xT.rearrange("(g p t) c -> g p t c", p=P, t=PACK)

        w_rows = w1.rearrange("(g p t) n -> g p t n", p=P, t=PACK)
        w_raw = [sbuf("w_raw%d" % g, [P, PACK, N], F32) for g in range(PASSES)]
        nc.scalar.dma_start(w_raw[0][:], w_rows[0])
        nc.sync.dma_start(offs_t[:], offs)
        nc.sync.dma_start(cls_t[:], cls)
        plane = {}
        for g, t0, rows in [(0, 0, 4), (1, 0, 3), (1, 3, 1)]:
            x_raw = sbuf("x_raw%d_%d" % (g, t0), [P, rows * T], F32)
            nc.sync.dma_start(x_raw[:], x_rows[g, :, t0 : t0 + rows, :].rearrange("p t c -> p (t c)"))
            for i in range(rows):
                plane[g, t0 + i] = x_raw[:, i * T : (i + 1) * T]
        nc.sync.dma_start(w_raw[1][:], w_rows[1])
        g_raw = [sbuf("g_raw%d" % b, [P, U], F32) for b in range(BLOCKS)]
        b_raw = [sbuf("b_raw%d" % b, [P, U], F32) for b in range(BLOCKS)]
        for raw, table in ((g_raw, gamma), (b_raw, beta)):
            for b in range(BLOCKS):
                nc.sync.dma_start(raw[b][:], table[b * P : (b + 1) * P, :])

        w_codes = {}
        w_scales = {}

        def quantise_w(g, b):
            w_bf = sbuf("w_bf%d_%d" % (g, b), [P, P, PACK], BF16)
            w_codes[g, b] = sbuf("w_codes%d_%d" % (g, b), [P, P], U32)
            w_scales[g, b] = sbuf("w_scales%d_%d" % (g, b), [P, P], U8)
            interleave(nc.scalar.copy, w_bf[:], w_raw[g][:, :, b * P : (b + 1) * P])
            nc.vector.quantize_mx(w_codes[g, b][:].bitcast(FP8X4), w_scales[g, b][:], w_bf[:].rearrange("p n t -> p (n t)"))

        for b in range(BLOCKS):
            quantise_w(0, b)

        x_bf = [sbuf("x_bf%d" % g, [P, S, PACK], BF16) for g in range(PASSES)]
        x_codes = {0: sbuf("x_codes0", [P, S], U32)}
        x_scales = [sbuf("x_scales%d" % g, [P, S], U8) for g in range(PASSES)]
        acc = {}
        for b in range(BLOCKS):
            for h in range(HALVES):
                acc[b, h] = psum.tile([P, H], F32, name="acc%d_%d" % (b, h))

        def quantise_x(g, h):
            nc.vector.quantize_mx(
                x_codes[g][:, half[h]].bitcast(FP8X4),
                x_scales[g][:, half[h]],
                x_bf[g][:, half[h], :].rearrange("p s t -> p (s t)"),
            )

        def multiply(g, b, h):
            nc.tensor.matmul_mx(
                out=acc[b, h][:],
                lhsT=w_codes[g, b][:].bitcast(FP8X4),
                lhsT_scale=w_scales[g, b][:],
                rhs=x_codes[g][:, half[h]].bitcast(FP8X4),
                rhs_scale=x_scales[g][:, half[h]],
                start=(g == 0),
                stop=(g == PASSES - 1),
            )

        picked = sbuf("picked", [P, PACK, S], F32)
        for t in range(2):
            nc.vector.tensor_copy(picked[:, t, :], plane[0, t].indirect(offs_t[:]))
            nc.scalar.activation(picked[:, 2 + t, :], plane[0, 2 + t].indirect(offs_t[:]), COPY)
        interleave(nc.vector.tensor_copy, x_bf[0][:, half[0], :], picked[:, :, half[0]])
        interleave(nc.scalar.copy, x_bf[0][:, half[1], :], picked[:, :, half[1]])
        for h in range(HALVES):
            quantise_x(0, h)
            for b in range(BLOCKS):
                multiply(0, b, h)

        late = sbuf("late", [P, PACK, H], F32)
        shares = [(slice(0, X_WOVEN_BY_SCALAR), nc.scalar.copy), (slice(X_WOVEN_BY_SCALAR, H), nc.vector.tensor_copy)]
        pair = sbuf("pair", [P, 2, H], F32)
        for t in range(PACK):
            gathered = pair[:, t, :] if t < 2 else x_bf[1][:, half[0], t]
            nc.vector.tensor_copy(gathered, plane[1, t].indirect(entries(offs_t, half[0])))
            if t == 2:
                nc.vector.tensor_copy(x_bf[1][:, half[0], 0:2], pair[:].rearrange("p t s -> p s t"))
            for part in [part for part, copy in shares] if t == PACK - 1 else [slice(0, H)]:
                listed = slice(H + part.start, H + part.stop)
                nc.scalar.activation(late[:, t, part], plane[1, t].indirect(entries(offs_t, listed)), COPY)
        for part, copy in shares:
            interleave(copy, x_bf[1][:, H + part.start : H + part.stop, :], late[:, :, part])
        x_codes[1] = sbuf("x_codes1", [P, S], U32, "x_raw1_3")
        for h in range(HALVES):
            quantise_x(1, h)
        for b in range(BLOCKS):
            quantise_w(1, b)
            for h in range(HALVES):
                multiply(1, b, h)

        scaled = [sbuf("scaled%d" % b, [P, S], F32) for b in range(BLOCKS)]
        for b in range(BLOCKS):
            g_picked = sbuf("g_picked%d" % b, [P, S], F32)
            for h in range(HALVES):
                cut = h * H + G_SCALAR[b][h]
                plain, rest = slice(h * H, cut), slice(cut, (h + 1) * H)
                nc.scalar.activation(g_picked[:, plain], g_raw[b][:].indirect(entries(cls_t, plain)), COPY)
                if cut < rest.stop:
                    nc.vector.tensor_copy(g_picked[:, rest], g_raw[b][:].indirect(entries(cls_t, rest)))
            for h in range(HALVES):
                nc.vector.tensor_tensor(scaled[b][:, half[h]], acc[b, h][:], g_picked[:, half[h]], MULT)

        for b, cuts in enumerate(B_FUSED):
            fused = [slice(lo, hi) for lo, hi in zip((0,) + cuts, cuts)]
            rest = slice(cuts[-1], S)
            rows = slice(b * P, (b + 1) * P)
            b_picked = sbuf("b_picked%d" % b, [P, S - rest.start], F32)
            nc.scalar.activation(b_picked[:], b_raw[b][:].indirect(entries(cls_t, rest)), COPY)
            result = sbuf("result%d" % b, [P, S], F32)
            for part in fused:
                nc.vector.tensor_tensor(result[:, part], b_raw[b][:].indirect(entries(cls_t, part)), scaled[b][:, part], ADD)
                if b == BLOCKS - 1:
                    nc.sync.dma_start(out[rows, part], result[:, part])
            nc.vector.tensor_tensor(result[:, rest], b_picked[:], scaled[b][:, rest], ADD)
            stored = rest if b == BLOCKS - 1 else slice(0, S)
            nc.sync.dma_start(out[rows, stored], result[:, stored])
